import numpy as np, ml_dtypes
CORES = [35,38,43,46]
N = 4
BF = ml_dtypes.bfloat16
def gentries(a):
    return np.ascontiguousarray(a.reshape(8, 16, -1).transpose(0, 2, 1)).reshape(8, -1)
def gtable(e):
    e = np.asarray(e); return np.ascontiguousarray(e.reshape(8, -1, 16).transpose(0, 2, 1)).reshape(128, -1).astype(np.int32)
R, H, LO, UP, SW = 384, 64, 3, 6, 3
S, M, T = LO + 1 + UP, N * R, R + (N - 1) * H
def byrank(v):
    return np.ascontiguousarray(v.reshape(8, -1, R, N).transpose(3, 0, 1, 2)).reshape(N, 8, -1)
def ships(rng, rows):
    return np.argsort(rng.random((N, 8, N - 1, rows)), axis=-1)[..., :H]
def users(rng, low):
    u = np.full((8, M), -1, np.int64)
    for g in range(8):
        for t in rng.permutation(LO):
            o = rng.permutation(M); l = low[g, t, o]; ok = l >= 0; u[g, l[ok]] = o[ok]
    return u
def grow(rng, ship, far, drop=0.05, sweep=False):
    G = np.arange(8)[:, None]; i = np.arange(M); q = i % N; n = i // N; K = (N - 1) * H
    low = np.empty((8, LO, M), np.int64); spot = np.empty((8, LO, M), np.int64); up = np.empty((8, UP, M), np.int64)
    for t in range(LO):
        e = rng.integers(0, K, (8, M))
        if sweep: e = np.where(n >= R // 2, ((n - R // 2) * LO + t) % K, e)
        b = e // H; p = b + (b >= q); k = ship[p, G, q - (q > p), e % H] * N + p
        take = (rng.random((8, M)) < far) & (k < i); own = (rng.random((8, M)) * n).astype(np.int64)
        c = np.where(take, k, own * N + q); none = (~take & (n == 0)) | (rng.random((8, M)) < drop)
        for s in range(t): none |= c == low[:, s]
        low[:, t] = np.where(none, -1 - t, c); spot[:, t] = np.where(none, rng.integers(0, T, (8, M)), np.where(take, R + e, own))
    u = users(rng, low); cand = []
    for x in (u, users(rng, low)):
        v = np.maximum(x, 0); l = low[G, rng.integers(0, LO, (8, M)), v]
        cand += [x, np.where((x >= 0) & (l > i), l, -1), np.where(x >= 0, u[G, v], -1)]
    cand = np.stack(cand); turn = rng.integers(0, UP, (8, M))
    for w in range(UP):
        c = cand[(w + turn) % UP, G, i]; other = i + 1 + (rng.random((8, M)) * (M - 1 - i)).astype(np.int64)
        good = (c > i) & (rng.random((8, M)) < 0.85)
        for s in range(w): good &= c != up[:, s]
        c = np.where(good, c, other); none = (c >= M) | (rng.random((8, M)) < 0.04)
        for s in range(w): none |= c == up[:, s]
        up[:, w] = np.where(none, M + w, c)
    return low, spot, up
def fill(rng, ship, low, spot, up):
    c = np.concatenate([low, np.broadcast_to(np.arange(M), (8, 1, M)), up], 1); real = byrank((c >= 0) & (c < M)).reshape(N, 8, 1, S, R)
    v = (0.03 + 0.09 * rng.random((N, 8, 16, S, R))) * (2 * rng.integers(0, 2, (N, 8, 16, S, R)) - 1)
    v = np.where(real, v, 0.0); v[:, :, :, LO] = 0.75 + 0.75 * rng.random((N, 8, 16, R))
    return {"val": v.reshape(N, 128, S * R).astype(BF), "col": byrank(c).astype(np.int32), "spot": np.stack([gtable(x) for x in byrank(spot)]), "ship": np.stack([gtable(x.reshape(8, -1)) for x in ship])}
def setup_inputs(rng):
    ship = ships(rng, R); return fill(rng, ship, *grow(rng, ship, 0.8))
def setup_inputs_halo(rng):
    ship = ships(rng, R // 2); return fill(rng, ship, *grow(rng, ship, 1.0, 0.0, True))
def setup_inputs_hub(rng):
    ship = rng.integers(0, 3, (N, 8, N - 1, H)); return fill(rng, ship, *grow(rng, ship, 0.95))
def setup_inputs_thin(rng):
    ship = ships(rng, R); low, spot, up = grow(rng, ship, 0.8)
    gone = rng.random((8, 1, M)) < rng.permutation(np.array([1.0, 1.0, 0.95, 0.8, 0.5, 0.5, 0.1, 0.0]))[:, None, None]
    gone = gone | (np.arange(M) % N == rng.integers(0, N))
    low = np.where(gone, -1 - np.arange(LO)[:, None], low); up = np.where(gone, M + np.arange(UP)[:, None], up)
    return fill(rng, ship, low, spot, up)
def setup_inputs_band(rng):
    ship = ships(rng, R); low, spot, up = grow(rng, ship, 0.8); n = np.arange(M) // N; q = np.arange(M) % N
    for g in range(6):
        for t in range(LO):
            b = n - (t + 1) * (g + 1); low[g, t] = np.where(b >= 0, b * N + q, -1 - t); spot[g, t] = np.where(b >= 0, b, 0)
        for w in range(UP):
            b = n + (w + 1) * (g + 1); up[g, w] = np.where(b < R, b * N + q, M + w)
    d = fill(rng, ship, low, spot, up); v = np.sign(d["val"].astype(np.float32)).reshape(N, 8, 16, S, R) * (0.125 - rng.integers(0, 4, (N, 8, 16, S, R)) * 2.0 ** -11)
    v[:, :, :, LO] = rng.choice(np.array([0.75, 0.75390625, 1.4921875, 1.5]), (N, 8, 16, R)); d["val"] = v.reshape(N, 128, S * R).astype(np.float32).astype(BF); return d
def setup_inputs_spread(rng):
    d = setup_inputs(rng); k = np.exp2(rng.integers(-6, 1, (N, 8, 1, S, R))) * (rng.random((N, 8, 1, S, R)) > 0.0625); k[:, :, :, LO] = 1
    d["val"] = (d["val"].astype(np.float32).reshape(N, 8, 16, S, R) * k).reshape(N, 128, S * R).astype(BF); return d
def check_inputs(d):
    bad = []; i = np.arange(R)[None] * N + np.arange(N)[:, None]; row = i[:, None, None]
    c = d["col"].astype(np.int64).reshape(N, 8, S, R); lo, up = c[:, :, :LO], c[:, :, LO + 1:]
    elo = lo == -1 - np.arange(LO)[:, None]; eup = up == M + np.arange(UP)[:, None]
    if not (c[:, :, LO] == i[:, None]).all(): bad.append("the diagonal's column is the row's number")
    if not (elo | ((lo >= 0) & (lo < row))).all(): bad.append("lower columns are below the row's number, or the slot is empty")
    if not (eup | ((up > row) & (up < M))).all(): bad.append("upper columns are above the row's number, or the slot is empty")
    s = np.sort(c, axis=2)
    if (s[:, :, 1:] == s[:, :, :-1]).any(): bad.append("the columns of a row differ")
    v = d["val"].astype(np.float32).reshape(N, 8, 16, S, R); e = np.concatenate([elo, np.zeros((N, 8, 1, R), bool), eup], 2)[:, :, None]
    if not ((v[:, :, :, LO] >= 0.75) & (v[:, :, :, LO] <= 1.5)).all(): bad.append("diagonals lie from 0.75 to 1.5")
    if not (np.abs(np.delete(v, LO, 3)) <= 0.125).all(): bad.append("other values are at most 0.125 in size")
    if not ((v == 0) | ~e).all(): bad.append("empty slots have the value 0")
    sh = np.stack([gentries(x) for x in d["ship"]]).astype(np.int64).reshape(N, 8, N - 1, H); sp = np.stack([gentries(x) for x in d["spot"]]).astype(np.int64)
    if not ((sh >= 0) & (sh < R)).all(): bad.append("ship names local rows")
    if not ((sp >= 0) & (sp < T)).all(): bad.append("spot holds places")
    for q in range(N):
        tab = np.concatenate([np.broadcast_to(i[q], (8, R))] + [sh[p][:, q - (q > p)] * N + p for p in range(N) if p != q], 1)
        k = np.take_along_axis(tab, np.clip(sp[q], 0, T - 1), 1).reshape(8, LO, R)
        if not ((k == lo[q]) | elo[q]).all(): bad.append("the row at a lower slot's place is its column"); break
    return bad
def reference(val, col, spot, ship):
    c = col.astype(np.int64).reshape(N, 8, S, R).transpose(1, 2, 3, 0).reshape(8, S, M)
    a = val.astype(np.float64).reshape(N, 8, 16, S, R).transpose(1, 2, 3, 4, 0).reshape(8, 16, S, M)
    y = np.empty((8, 16, S, M)); z = np.empty((8, 16, M))
    for g in range(8):
        k = np.maximum(c[g, :LO], 0)
        at = np.full((S, LO, M), UP * M, np.int64)
        for w in range(UP): at = np.where(c[g, LO + 1 + w][k][None] == c[g][:, None], w * M + k[None], at)
        x = a[g]; r = np.ones((16, M))
        for sweep in range(SW):
            u = np.concatenate([x[:, LO + 1:].reshape(16, UP * M), np.zeros((16, 1))], 1); d = np.array(a[g])
            for t in range(LO): d -= x[:, t][:, None] * u[:, at[:, t]]
            for t in range(LO): d[:, t] *= r[:, k[t]]
            r = r * (2 - x[:, LO] * r); x = d
        y[g] = x; z[g] = r
    y = y.reshape(8, 16, S, R, N).transpose(4, 0, 1, 2, 3).reshape(N, 128, S * R); z = z.reshape(8, 16, R, N).transpose(3, 0, 1, 2).reshape(N, 128, R)
    return {"y": y.astype(np.float32), "inv": z.astype(np.float32)}

@@ -1,0 +1,490 @@
+from concourse.bass import DstId, RemoteDMATransfer
+from concourse.mybir import AluOpType, ActivationFunctionType
+
+R, H, NB = 384, 64, 3
+HB = 8 * R
+HS = 8 * H
+WN = HB + NB * HS
+ZC = R + NB * H
+NP = 5
+NPE = {1: (2, 2, 2, 2, 1, 1), 2: (2, 2, 2, 2, 1, 1), 3: (2, 2, 2, 2, 1, 1)}
+
+
+def _sb(dtype, **shapes):
+    return {k: ("sbuf", [128] + list(v), dtype) for k, v in shapes.items()}
+
+
+SCRATCH = {}
+SCRATCH.update(_sb("int32", colraw=[R], shp=[12], spt=[72], pi=[1], pt=[2], nvi=[72], ki=[72], sps=[72], blk=[72],
+                   ts=[72], cs=[72]))
+SCRATCH.update(_sb("uint16", shp16=[12], vl=[84], lb=[24], list2=[144], prm=[72], unperm=[72], rl1=[72], rl2=[72], ls=[576]))
+SCRATCH.update(_sb("float16", in2=[24, 32], t2=[24, 32], c3=[72, 9], idh=[128]))
+SCRATCH.update(_sb("bfloat16", vsend=[NB * 7 * H], eq=[576, 6], ones=[128], idb=[128], idw=[6 * 128], al=[3 * R],
+                   als=[3 * R], w1=[WN]))
+SCRATCH.update(_sb("float32", stg=[3, 7, 4], cw=[ZC + 8], csend=[NB * H], pf=[8], shpf=[12], sptf=[72], ext=[120],
+                   cmpx=[96], nvf=[72], kk=[72], spf=[72], srt=[72], tmp=[72], tsf=[72], strd=[72], base=[72], ta=[72],
+                   tb=[72], istr=[72], bq=[72], rl=[72], fin=[576], rk2=[72], rk3=[72], gu=[72 * 32], tu=[72, 32],
+                   upc=[432], neg=[128], idf=[128], w2=[WN], w3=[WN], r1=[R], rw=[ZC], r3=[R], rsend=[NB * H],
+                   rj1=[3 * R], rj2=[3 * R], l3=[3 * R], gg=[24 * R], pp=[NP * 3 * R], snd2=[NB * 6 * H],
+                   snd3=[NB * 6 * H], yy=[10 * R]))
+SCRATCH["xl"] = ("psum", [128, 1536], "float32")
+for _i in range(5):
+    SCRATCH["a%d" % _i] = ("psum", [128, 512], "float32")
+ARR = ["c0", "v0", "r2"] + ["x%d%d" % (k, i) for k in (2, 3) for i in range(3)]
+SEMAPHORES = ["v", "s", "t", "g", "sent"] + ["a_" + a for a in ARR] + ["d%d" % i for i in range(16)]
+
+
+def rank_program(g, core, T, topo):
+    rank = T.rank_of(core)
+    if rank is None:
+        return
+    A = AluOpType
+    F = ActivationFunctionType
+    N = len(T.cores)
+    Q = {"v": g.vector, "s": g.scalar, "t": g.tensor, "g": g, "y": g.sync}
+    cnt = {"v": 0, "s": 0, "t": 0, "g": 0, "sent": 0, "d": 0}
+    clock = {q: {} for q in Q}
+    writer, readers = {}, {}
+
+    def wait(q, tok):
+        sem, n, clk = tok[0], tok[1], tok[2]
+        c = clock[q]
+        if c.get(sem, 0) >= n:
+            return
+        Q[q].wait_ge(T.sem[sem], n)
+        c[sem] = n
+        for k in clk:
+            if c.get(k, 0) < clk[k]:
+                c[k] = clk[k]
+
+    def before(q, rd, wr, dma):
+        need = []
+        for k in rd:
+            if k in writer:
+                need.append(writer[k])
+            if k[0] == "P":
+                need += [t for t in readers.get(k, []) if t[3] != q]
+        for k in wr:
+            if k in writer and (dma or writer[k][3] != q):
+                need.append(writer[k])
+            need += readers.get(k, [])
+        need.sort(key=lambda t: -t[1])
+        for t in need:
+            wait(q, t)
+
+    def after(tok, rd, wr):
+        for k in rd:
+            readers.setdefault(k, []).append(tok)
+        for k in wr:
+            writer[k] = tok
+            readers[k] = []
+
+    def op(q, call, rd, wr):
+        before(q, rd, wr, False)
+        cnt[q] += 1
+        call().then_inc(T.sem[q], 1)
+        after((q, cnt[q], dict(clock[q]), q), rd, wr)
+
+    def mm(calls, rd, wr, each=False):
+        before("t", rd, wr, False)
+        for i, (o, l, r) in enumerate(calls):
+            ins = g.tensor.matmul(o, l, r, each or i == 0, each or i == len(calls) - 1)
+        cnt["t"] += 1
+        ins.then_inc(T.sem.t, 1)
+        after(("t", cnt["t"], dict(clock["t"]), "t"), rd, wr)
+
+    def dma(q, out, in_, rd, wr):
+        before(q, rd, wr, True)
+        sem = "d%d" % cnt["d"]
+        cnt["d"] += 1
+        Q[q].dma_start(out, in_).then_inc(T.sem[sem], 16)
+        after((sem, 16, dict(clock[q]), "dma"), rd, wr)
+
+    def plan(src):
+        dsts = [c for c in T.cores if c != src]
+        far = [c for c in dsts if topo.chip(c) != topo.chip(src)]
+        near = [c for c in dsts if c not in far]
+        used, out = [], {}
+        for grp in (far, near):
+            if not grp:
+                continue
+            free = [e for e in topo.engines(src, grp[0]) if e not in used]
+            n = 4
+            while n * len(grp) > len(free):
+                n //= 2
+            step = len(free) // n
+            for i, c in enumerate(grp):
+                out[c] = free[i::step][:n]
+            used += free
+        return out
+
+    mine = plan(core)
+    others = [p for p in range(N) if p != rank]
+    arrive = sum(len(plan(T.cores[p])[core]) for p in others)
+
+    def send(name, src, width, dst, rd):
+        before("g", rd, [], True)
+        tr = []
+        for b, p in enumerate(others):
+            c = T.cores[p]
+            rid, pid = topo.addr(c)[0:2]
+            me = rank if rank < p else rank - 1
+            m = sum(1 << e for e in mine[c])
+            tr.append(RemoteDMATransfer(dst_ids=[DstId(rid=rid, pnc=pid)], dma_engine_mask=m,
+                                        remote_sem=T.sem["a_" + name], src=src(b * width, (b + 1) * width), dst=dst(me)))
+            cnt["sent"] += len(mine[c])
+        g.remote_dma_fused(tr, local_sem=T.sem.sent)
+
+    for a in ARR:
+        writer["arr." + a] = ("a_" + a, arrive, {}, "far")
+
+    V, S = g.vector, g.scalar
+
+    def tt(out, a, b, o, rd, wr):
+        op("v", lambda: V.tensor_tensor(out, a, b, o), rd, wr)
+
+    def ts(out, a, s1, s2, o0, o1, rd, wr):
+        if o1 is None:
+            op("v", lambda: V.tensor_scalar(out, a, s1, None, o0), rd, wr)
+        else:
+            op("v", lambda: V.tensor_scalar(out, a, s1, s2, o0, o1), rd, wr)
+
+    def cp(out, a, rd, wr):
+        op("v", lambda: V.tensor_copy(out, a), rd, wr)
+
+    def act(out, a, rd, wr, scale=1.0, bias=0.0):
+        if scale == 1.0 and bias == 0.0:
+            op("s", lambda: S.activation(out, a, F.Copy), rd, wr)
+        else:
+            op("s", lambda: S.activation(out, a, F.Identity, bias=bias, scale=scale), rd, wr)
+
+    def third(buf, t):
+        return buf[:, 24 * t:24 * t + 24]
+
+    dma("y", T.shp[:], T.ship[:], [], ["shp"])
+    dma("s", T.colraw[1:128:2, :], T.col[:, 0:8 * R], [], ["colB"])
+    dma("y", T.colraw[0:128:2, :], T.col[:, 2 * R:10 * R], [], ["colA"])
+    dma("s", T.spt[:], T.spot[:], [], ["spt"])
+    dma("y", T.w1[:, R:HB], T.val[:, 3 * R:10 * R], [], ["w1.own"])
+    dma("y", T.al[:], T.val[:, 0:3 * R], [], ["al"])
+
+    op("g", lambda: g.iota(T.pi[:], [[0, 1]], 0, 1), [], ["pi"])
+    op("g", lambda: g.iota(T.nvi[:], [[0, 3], [16, 24]], 0, 1), [], ["nvi"])
+    op("v", lambda: V.memset(T.ones[:], 1.0), [], ["ones"])
+    op("g", lambda: g.affine_select(T.idb[:], T.ones[:], [[-1, 128]], A.is_equal, 0.0, 0, 1), ["ones"], ["idb"])
+    op("v", lambda: V.memset(T.cw[:, ZC:ZC + 8], 0.0), [], ["cw.z"])
+    op("v", lambda: V.memset(T.w1[:, 0:R], 0.0), [], ["w1.z0"])
+    for b in range(NB):
+        op("v", lambda: V.memset(T.w1[:, HB + b * HS:HB + b * HS + H], 0.0), [], ["w1.z%d" % (b + 1)])
+    ts(T.pt[:, 0:1], T.pi[:], 4, None, A.logical_shift_right, None, ["pi"], ["pt0"])
+    ts(T.pt[:, 1:2], T.pi[:], 4, 1, A.logical_shift_right, A.bitwise_and, ["pi"], ["pt1"])
+    M0, M1, Z0, Z1, PH = [T.pf[:, i:i + 1] for i in range(5)]
+    ts(PH, T.pt[:, 0:1], 16.0, None, A.mult, None, ["pt0"], ["ph"])
+    ts(M0, T.pt[:, 1:2], -1.0, 1.0, A.mult, A.add, ["pt1"], ["m0"])
+    ts(M1, T.pt[:, 1:2], 1.0, None, A.mult, None, ["pt1"], ["m1"])
+    ts(Z0, T.pt[:, 1:2], float(ZC), None, A.mult, None, ["pt1"], ["z0"])
+    ts(Z1, T.pt[:, 1:2], -float(ZC), float(ZC), A.mult, A.add, ["pt1"], ["z1"])
+    ts(T.nvf[:], T.nvi[:], PH, 1.0 / R, A.subtract, A.mult, ["nvi", "ph"], ["nvf"])
+    cp(T.idh[:], T.idb[:], ["idb"], ["idh"])
+    act(T.idf[:], T.idb[:], ["idb"], ["idf"])
+    act(T.neg[:], T.idb[:], ["idb"], ["neg"], scale=-1.0)
+    for w in range(6):
+        act(T.idw[:, w * 128:(w + 1) * 128], T.idb[:], ["idb"], ["idw%d" % w], scale=float(w + 2))
+
+    col = ["colA", "colB"]
+    cp(T.shp16[:], T.shp[:], ["shp"], ["shp16"])
+    cp(T.shpf[:], T.shp[:], ["shp"], ["shpf"])
+    cp(T.sptf[:], T.spt[:], ["spt"], ["sptf"])
+    cp(T.csend[:], T.colraw[:, 0:R].indirect(T.shp16[:, 0:12]), col + ["shp16"], ["csend"])
+    send("c0", lambda a, b: T.csend[:, a:b], H, lambda b: T.cw[:, R + b * H:R + (b + 1) * H], ["csend"])
+    stg = ["stg%d" % w for w in range(7)]
+    for t in range(3):
+        act(third(T.spf, t), third(T.sptf, t), ["sptf"], ["spf%d" % t], scale=1.0 / 1024, bias=3.0 + t / 4096.0)
+    for w in range(7):
+        act(T.stg[:, :, w, :], T.shpf[:], ["shpf"], [stg[w]], bias=float(w * R))
+
+    ts(T.in2[:, :, 0:16], T.colraw[:], M0, None, A.mult, None, col + ["m0"], ["in2a"])
+    ts(T.in2[:, :, 16:32], T.colraw[:], M1, None, A.mult, None, col + ["m1"], ["in2b"])
+    cp(T.cw[:, 0:R], T.colraw[:], col, ["cw.own"])
+    op("v", lambda: V.transpose(T.t2[:], T.in2[:]), ["in2a", "in2b"], ["t2"])
+    cp(T.vl[:], T.stg[:], stg, ["vl"])
+    act(T.vsend[:], T.w1[:, R:HB].indirect(T.vl[:, 0:84]), ["w1.own", "vl"], ["vsend"])
+    send("v0", lambda a, b: T.vsend[:, a:b], 7 * H, lambda b: T.w1[:, HB + b * HS + H:HB + (b + 1) * HS], ["vsend"])
+    for k, W in ((2, T.w2), (3, T.w3)):
+        op("g", lambda: g.iota(W[:, 0:2 * R], [[0, 2 * R]], 0, 0, allow_small_or_imprecise_dtypes=True), [], ["w%d.z0" % k])
+        for b in range(NB):
+            op("g", lambda: g.iota(W[:, HB + b * HS:HB + b * HS + 2 * H], [[0, 2 * H]], 0, 0,
+                                   allow_small_or_imprecise_dtypes=True), [], ["w%d.z%d" % (k, b + 1)])
+    for t in range(3):
+        tt(third(T.kk, t), T.t2[:, :, 2 * t + 1], T.t2[:, :, 2 * t + 17], A.add, ["t2"], ["kk%d" % t])
+    tt(T.c3[:, 0:24, 0:7], T.t2[:, :, 2:16:2], T.t2[:, :, 18:32:2], A.add, ["t2"], ["c30"])
+    tt(T.ext[:, 24:96], T.kk[:], T.spf[:], A.add, ["kk0", "kk1", "kk2", "spf0", "spf1", "spf2"], ["key"])
+    k0, k1, k2 = [third(T.ext, t + 1) for t in range(3)]
+    s0, s1, s2 = [third(T.srt, t) for t in range(3)]
+    m0, m1, m2 = [third(T.tmp, t) for t in range(3)]
+    tt(m1, k0, k1, A.max, ["key"], ["tm1"])
+    tt(m0, k0, k1, A.min, ["key"], ["tm0"])
+    tt(m2, m1, k2, A.min, ["tm1", "key"], ["tm2"])
+    tt(s0, m0, k2, A.min, ["tm0", "key"], ["s0"])
+    tt(s2, m1, k2, A.max, ["tm1", "key"], ["s2"])
+    tt(s1, m0, m2, A.max, ["tm0", "tm2"], ["s1"])
+    ts(T.ki[:], T.srt[:], 4096.0, None, A.mult, None, ["s0", "s1", "s2"], ["ki"])
+    ts(T.sps[:], T.ki[:], 2, 1023, A.logical_shift_right, A.bitwise_and, ["ki"], ["sps"])
+    ts(T.cs[:], T.ki[:], 12, None, A.logical_shift_right, None, ["ki"], ["cs"])
+    ts(T.list2[:, 0:144:2], T.sps[:], M0, Z0, A.mult, A.add, ["sps", "m0", "z0"], ["l2a"])
+    ts(T.list2[:, 1:144:2], T.sps[:], M1, Z1, A.mult, A.add, ["sps", "m1", "z1"], ["l2b"])
+
+    cwk = ["cw.own", "cw.z", "arr.c0", "l2a", "l2b"]
+    for j in range(3):
+        act(T.gu[:, 768 * j:768 * j + 768], T.cw[:, 0:ZC + 8].indirect(T.list2[:, 48 * j:48 * j + 48]), cwk, ["gu%d" % j])
+    ts(T.c3[:, 0:24, 7], third(T.cs, 1), -3.0, None, A.add, None, ["cs"], ["c31"])
+    ts(T.c3[:, 0:24, 8], third(T.cs, 2), -3.0, None, A.add, None, ["cs"], ["c32"])
+    ts(T.ts[:], T.ki[:], 3, None, A.bitwise_and, None, ["ki"], ["ts"])
+    ts(T.blk[:], T.ki[:], 8, 15, A.logical_shift_right, A.bitwise_and, ["ki"], ["blk"])
+    cr = ["c30", "c31", "c32"]
+    cp(T.c3[:, 24:48, :], T.c3[:, 0:24, :], cr, ["c33"])
+    cp(T.c3[:, 48:72, :], T.c3[:, 0:24, :], cr, ["c34"])
+    cr += ["c33", "c34"]
+    tt(T.tsf[:], T.ts[:], T.nvf[:], A.add, ["ts", "nvf"], ["tsf"])
+    ts(T.ta[:], T.blk[:], 6.0, float(HS - H), A.is_ge, A.mult, ["blk"], ["ta"])
+    ts(T.tb[:], T.blk[:], 6.0, float(H - R), A.is_ge, A.mult, ["blk"], ["tb"])
+    ts(T.prm[:], T.tsf[:], float(R), 0.25, A.mult, A.add, ["tsf"], ["prm"])
+    act(T.als[:], T.al[:, 0:3 * R].indirect(T.prm[:, 0:72]), ["al", "prm"], ["als"])
+    act(T.r1[:], T.w1[:, R:2 * R], ["w1.own"], ["r1"], scale=-1.0, bias=2.0)
+    act(T.ext[:, 0:24], k2, ["key"], ["ext0"])
+    act(T.ext[:, 96:120], k0, ["key"], ["ext1"])
+    tt(T.ta[:], T.ta[:], T.blk[:], A.mult, ["ta", "blk"], ["ta"])
+    ts(T.strd[:], T.tb[:], float(R), None, A.add, None, ["tb"], ["strd"])
+    ts(T.istr[:], T.tb[:], (1.0 / H - 1.0 / R) / (H - R), 1.0 / R, A.mult, A.add, ["tb"], ["istr"])
+    tt(T.base[:], T.ta[:], T.sps[:], A.add, ["ta", "sps"], ["base"])
+    cp(T.lb[:], T.stg[:, :, 0:2, :], stg, ["lb"])
+    tt(T.bq[:], T.base[:], T.istr[:], A.mult, ["base", "istr"], ["bq"])
+    cp(T.rl2[:], T.sps[:], ["sps"], ["rl2"])
+
+    ACC = [T.a0, T.a1, T.a2, T.a3, T.a4]
+
+    def cbank(i):
+        return (T.xl, 512 * i, "Pxl") if i < 3 else (ACC[(0, 1, 4)[i % 3]], 0, "Pa%d" % (0, 1, 4)[i % 3])
+
+    def spread(i):
+        s = (i + 1 if i < 6 else 0) if i < 7 else 15 - i
+        n = 72 if i < 7 else 24 * (9 - i)
+        B, o, bk = cbank(i)
+        mm([(B[:, o + w:o + 6 * n:6], T.idh[:], T.c3[:, 0:n, s]) for w in range(6)], cr + ["idh"], [bk], True)
+
+    for i in range(6):
+        spread(i)
+    for j in range(3):
+        op("v", lambda: V.transpose(T.tu[:, 24 * j:24 * j + 24, :], T.gu[:, 768 * j:768 * j + 768]), ["gu%d" % j], ["tu%d" % j])
+        if j == 0:
+            tt(T.rl[:], T.base[:], T.strd[:], A.add, ["base", "strd"], ["rl"])
+        for i in ((), (0,), (1, 2))[j]:
+            tt(T.upc[:, 144 * i:144 * i + 144], T.tu[:, 24 * i:24 * i + 24, 4:16:2], T.tu[:, 24 * i:24 * i + 24, 20:32:2],
+               A.add, ["tu%d" % i], ["upc%d" % i])
+    cp(T.rl1[:], T.rl[:], ["rl"], ["rl1"])
+
+    def compare(i):
+        n = 72 if i < 7 else 24 * (9 - i)
+        o = 72 * i if i < 8 else 552
+        B, c, bk = cbank(i)
+        tt(T.eq[:, o:o + n, :], B[:, c:c + 6 * n], T.upc[:, 0:6 * n], A.is_equal, [bk, "upc0", "upc1", "upc2"], ["eq%d" % i])
+
+    PARTS = [((0, 72), (72, 72))] * 3 + [((0, 72), (72, 48), (120, 24))]
+
+    def weigh(lg):
+        B = ACC[2 + lg % 2]
+        e = ["eq%d" % i for i in ((2 * lg, 2 * lg + 1) if lg < 3 else (6, 7, 8))]
+        calls = [(B[:, 0:144], T.idw[:, w * 128:(w + 1) * 128], T.eq[:, 144 * lg:144 * lg + 144, w]) for w in range(6)]
+        calls += [(B[:, o:o + n], T.idf[:], T.bq[:, 0:n]) for o, n in PARTS[lg]]
+        mm(calls, e + ["idw%d" % w for w in range(6)] + ["idf", "bq"], ["Pa%d" % (2 + lg % 2)])
+
+    def final(lg, step):
+        if step == 0:
+            for o, n in PARTS[lg]:
+                tt(T.fin[:, 144 * lg + o:144 * lg + o + n], ACC[2 + lg % 2][:, o:o + n], T.strd[:, 0:n], A.mult,
+                   ["Pa%d" % (2 + lg % 2), "strd"], ["fin%d.%d" % (lg, o)])
+        else:
+            ts(T.ls[:, 144 * lg:144 * lg + 144], T.fin[:, 144 * lg:144 * lg + 144], 0.25, None, A.add, None,
+               ["fin%d.%d" % (lg, o) for o, n in PARTS[lg]], ["ls%d" % lg])
+
+    WIN = {1: T.w1, 2: T.w2, 3: T.w3}
+    WK = {1: ["w1.own", "arr.v0"] + ["w1.z%d" % i for i in range(4)]}
+    for k in (2, 3):
+        WK[k] = (["w%d.u%d" % (k, w) for w in range(6)] + ["w%d.z%d" % (k, i) for i in range(4)]
+                 + ["arr.x%d%d" % (k, i) for i in range(3)])
+    ITEM = [(3 * i, 3) for i in range(7)] + [(21, 2), (23, 1)]
+    st = {"p": 0, "a": 0, "keep": None}
+    held = {}
+
+    def gather(k, i, q="s", j0=0, j1=3):
+        o, n = ITEM[i]
+        j1 = min(j1, n)
+        (act if q == "s" else cp)(T.gg[:, (o + j0) * R:(o + j1) * R],
+                                  WIN[k][:, 0:WN].indirect(T.ls[:, 24 * (o + j0):24 * (o + j1)]),
+                                  WK[k] + ["ls%d" % min(i // 2, 3)], ["g%d" % (o + j) for j in range(j0, j1)])
+
+    def aval(i):
+        if i < 6:
+            return T.w1[:, (2 + i) * R:(3 + i) * R]
+        if i == 6:
+            return T.w1[:, R:2 * R]
+        return T.als[:, (9 - i) * R:(10 - i) * R]
+
+    def prod(p, j0, j1):
+        return T.pp[:, (p * 3 + j0) * R:(p * 3 + j1) * R]
+
+    def accumulate(i, npe):
+        if st["a"] % 5 == st["keep"]:
+            st["a"] += 1
+        a = st["a"] % 5
+        st["a"] += 1
+        calls = [(ACC[a][:, 0:R], T.idb[:], aval(i))]
+        rd = ["idb", "neg", "als", "w1.own"]
+        if not npe:
+            held[i] = [None, None, 0]
+        for j in range(npe):
+            calls.append((ACC[a][:, 0:R], T.neg[:], prod(held[i][0], j, j + 1)))
+            rd.append("p%d.%d" % (held[i][0], j))
+        mm(calls, rd, ["Pa%d" % a])
+        held[i][1] = a
+
+    def mult(i, npe, cut=False):
+        o, n = ITEM[i]
+        p = st["p"] % NP
+        st["p"] += 1
+        held[i] = [p, held[i][1] if npe is None else None, npe or 0]
+        for j0, j1 in (((0, npe), (npe, n)) if cut else ((0, n),)):
+            tt(prod(p, j0, j1), T.gg[:, (o + j0) * R:(o + j1) * R], T.xl[:, j0 * R:j1 * R], A.mult,
+               ["g%d" % (o + j) for j in range(j0, j1)] + ["Pxl"], ["p%d.%d" % (p, j) for j in range(j0, j1)])
+            if j0 == 0 and npe:
+                accumulate(i, npe)
+
+    def lessen(i):
+        p, a, j = held[i]
+        tt(ACC[a][:, 0:R], ACC[a][:, 0:R], prod(p, j, j + 1), A.subtract, ["Pa%d" % a, "p%d.%d" % (p, j)], ["Pa%d" % a])
+        held[i][2] = j + 1
+
+    def evict(i, out, key):
+        p, a, j = held[i]
+        tt(out, ACC[a][:, 0:R], prod(p, j, j + 1), A.subtract, ["Pa%d" % a, "p%d.%d" % (p, j)], [key])
+
+    def scale(i, rj, rk, out, ok):
+        a = held[i][1]
+        j = 9 - i
+        tt(out[:, j * R:(j + 1) * R], ACC[a][:, 0:R], rj[:, j * R:(j + 1) * R], A.mult, ["Pa%d" % a, rk], [ok])
+
+    def ship(k, c, q):
+        SB = T.snd2 if k == 2 else T.snd3
+        w0, o = 2 * c, NB * 2 * c * H
+        src = WIN[k][:, (2 + w0) * R:(4 + w0) * R].indirect(T.lb[:, 0:24])
+        key = "snd%d%d" % (k, c)
+        (act if q == "s" else cp)(SB[:, o:o + NB * 2 * H], src, ["w%d.u%d" % (k, w0), "w%d.u%d" % (k, w0 + 1), "lb"], [key])
+        send("x%d%d" % (k, c), lambda a, b: SB[:, o + a:o + b], 2 * H,
+             lambda b: WIN[k][:, HB + b * HS + (2 + w0) * H:HB + b * HS + (4 + w0) * H], [key])
+
+    def newton(step, r=None, rk=None, out=None, ok=None):
+        a = st["keep"]
+        P, pk = ACC[a][:, 0:R], "Pa%d" % a
+        if step == 0:
+            tt(P, P, r, A.mult, [pk, rk], [pk])
+        elif step == 1:
+            act(P, P, [pk], [pk], scale=-1.0, bias=2.0)
+        else:
+            tt(out, P, r, A.mult, [pk, rk], [ok])
+            st["keep"] = None
+
+    def uppers(k, mid, done, dst):
+        npe = NPE[k]
+        for w in range(7):
+            if w < 6:
+                mult(w, npe[w], npe[w] == 1 or w == 5)
+                if w in mid:
+                    mid[w]()
+            if w:
+                for _ in range(2 - npe[w - 1]):
+                    lessen(w - 1)
+                evict(w - 1, *dst(w - 1))
+                if w - 1 in done:
+                    done[w - 1]()
+
+    def up(k):
+        return lambda w: (WIN[k][:, (2 + w) * R:(3 + w) * R], "w%d.u%d" % (k, w))
+
+    compare(0); compare(1); weigh(0)
+    compare(2); compare(3); weigh(1); spread(6); final(0, 0); compare(4); spread(7); final(0, 1)
+    gather(1, 0); gather(1, 1)
+    compare(5); weigh(2); spread(8); final(1, 0); compare(6); final(1, 1)
+    gather(1, 2); gather(1, 3)
+    for o, n in ((0, 512), (512, 512), (1024, 128)):
+        mm([(T.xl[:, o:o + n], T.idb[:], T.als[:, o:o + n])], ["idb", "als"], ["Pxl"])
+    final(2, 0); compare(7); final(2, 1); compare(8); weigh(3)
+    gather(1, 4)
+    uppers(1, {0: lambda: final(3, 0), 1: lambda: final(3, 1)},
+           {1: lambda: (ship(2, 0, "s"), gather(1, 5), gather(1, 8), gather(1, 7)),
+            3: lambda: (ship(2, 1, "s"), gather(1, 6)),
+            5: lambda: ship(2, 2, "v")}, up(2))
+    act(T.rj1[:], T.w1[:, 0:WN].indirect(T.rl1[:, 0:72]), WK[1] + ["rl1"], ["rj1"], scale=-1.0, bias=2.0)
+    accumulate(8, 0); mult(7, 1); mult(8, None); mult(6, 3)
+    st["keep"] = held[6][1]
+    tt(T.cmpx[:], T.ext[:, 0:96], T.ext[:, 24:120], A.is_gt, ["key", "ext0", "ext1"], ["cmpx"])
+    evict(8, T.xl[:, R:2 * R], "Pxl")
+    tt(T.rk2[:], T.cmpx[:, 24:96], T.cmpx[:, 0:72], A.subtract, ["cmpx"], ["rk2"])
+    evict(7, T.xl[:, 2 * R:3 * R], "Pxl")
+    tt(T.rk3[:], T.rk2[:], T.nvf[:], A.add, ["rk2", "nvf"], ["rk3"])
+    ts(T.unperm[:], T.rk3[:], float(R), R + 0.25, A.mult, A.add, ["rk3"], ["unperm"])
+    newton(0, T.r1[:], "r1")
+    newton(1)
+
+    gather(2, 0, "v")
+    for i in range(1, 5):
+        gather(2, i)
+
+    def rsend():
+        act(T.rsend[:], T.rw[:, 0:R].indirect(T.shp16[:, 0:12]), ["rw.own", "shp16"], ["rsend"])
+        send("r2", lambda a, b: T.rsend[:, a:b], H, lambda b: T.rw[:, R + b * H:R + (b + 1) * H], ["rsend"])
+
+    uppers(2, {1: lambda: newton(2, T.r1[:], "r1", T.rw[:, 0:R], "rw.own")},
+           {1: lambda: (ship(3, 0, "s"), gather(2, 5), rsend()),
+            3: lambda: (ship(3, 1, "s"), gather(2, 8), gather(2, 7), gather(2, 6)),
+            5: lambda: ship(3, 2, "v")}, up(3))
+    act(T.rj2[:], T.rw[:, 0:ZC].indirect(T.rl2[:, 0:72]), ["rw.own", "arr.r2", "rl2"], ["rj2"])
+    accumulate(9, 0)
+    mult(8, 1); mult(7, 2); mult(6, 3)
+    st["keep"] = held[6][1]
+    scale(9, T.rj2, "rj2", T.l3, "l30")
+    scale(9, T.rj1, "rj1", T.xl, "Pxl")
+    scale(8, T.rj1, "rj1", T.xl, "Pxl")
+    scale(7, T.rj1, "rj1", T.xl, "Pxl")
+
+    def out(c0, c1, keys):
+        dma("y", T.y[:, c0:c1], T.yy[:, c0:c1], keys, ["y%d" % c0])
+
+    def ys(s):
+        return T.yy[:, s * R:(s + 1) * R], "yy%d" % s
+
+    gather(3, 7); gather(3, 6, "s", 1, 3)
+    gather(3, 8, "v"); gather(3, 6, "v", 0, 1)
+    mult(8, 1)
+    newton(0, T.rw[:, 0:R], "rw.own")
+    newton(1)
+    for i in (0, 1, 2, 3):
+        gather(3, i)
+    mult(7, 2)
+    scale(8, T.rj2, "rj2", T.l3, "l31")
+    mult(6, 2)
+    newton(2, T.rw[:, 0:R], "rw.own", T.r3[:], "r3")
+    dma("y", T.inv[:], T.r3[:], ["r3"], ["inv"])
+    scale(7, T.rj2, "rj2", T.l3, "l32")
+    act(T.yy[:, 0:3 * R], T.l3[:, 0:3 * R].indirect(T.unperm[:, 0:72]), ["l30", "l31", "l32", "unperm"], ["yyl"])
+    gather(3, 4)
+    gather(3, 5, "s", 0, 1); gather(3, 5, "s", 1, 3)
+    done = {w: (lambda w=w: out((4 + w) * R, (5 + w) * R, ["yy%d" % (4 + w)])) for w in range(6)}
+    uppers(3, {0: lambda: (evict(6, *ys(3)), out(3 * R, 4 * R, ["yy3"])), 4: lambda: out(0, 3 * R, ["yyl"])},
+           done, lambda w: ys(4 + w))
+
+    for q in ("v", "s", "t", "g", "sent"):
+        wait("g", (q, cnt[q], {}))
+    for a in ARR:
+        wait("g", ("a_" + a, arrive, {}))
+    for i in range(cnt["d"]):
+        wait("g", ("d%d" % i, 16, {}))

@@ -6,8 +6,18 @@ HB = 8 * R
 HS = 8 * H
 WN = HB + NB * HS
 ZC = R + NB * H
-NP = 5
-NPE = {1: (2, 2, 2, 2, 1, 1), 2: (2, 2, 2, 2, 1, 1), 3: (2, 2, 2, 2, 1, 1)}
+NP = 8
+CFG = {
+    "out": {1: "vvvvvv-", 2: "vvvvvv-", 3: "vvvvvvv"},
+    "eng": 4,
+    "cut": (0, 2, 4, 6),
+    "shipq": "sss",
+    "low": 6,
+    "newton": (("F", 1), ("S", 0)),
+    "lag1": dict(G=0, F=0, D=2, S=2, E=3),
+    "lag2": dict(G=0, F=0, D=2, S=2, E=3),
+    "lag3": dict(G=0, F=0, D=2, S=2, E=3),
+}
 
 
 def _sb(dtype, **shapes):
@@ -16,22 +26,24 @@ def _sb(dtype, **shapes):
 
 SCRATCH = {}
 SCRATCH.update(_sb("int32", colraw=[R], shp=[12], spt=[72], pi=[1], pt=[2], nvi=[72], ki=[72], sps=[72], blk=[72],
-                   ts=[72], cs=[72]))
-SCRATCH.update(_sb("uint16", shp16=[12], vl=[84], lb=[24], list2=[144], prm=[72], unperm=[72], rl1=[72], rl2=[72], ls=[576]))
-SCRATCH.update(_sb("float16", in2=[24, 32], t2=[24, 32], c3=[72, 9], idh=[128]))
-SCRATCH.update(_sb("bfloat16", vsend=[NB * 7 * H], eq=[576, 6], ones=[128], idb=[128], idw=[6 * 128], al=[3 * R],
-                   als=[3 * R], w1=[WN]))
-SCRATCH.update(_sb("float32", stg=[3, 7, 4], cw=[ZC + 8], csend=[NB * H], pf=[8], shpf=[12], sptf=[72], ext=[120],
-                   cmpx=[96], nvf=[72], kk=[72], spf=[72], srt=[72], tmp=[72], tsf=[72], strd=[72], base=[72], ta=[72],
-                   tb=[72], istr=[72], bq=[72], rl=[72], fin=[576], rk2=[72], rk3=[72], gu=[72 * 32], tu=[72, 32],
-                   upc=[432], neg=[128], idf=[128], w2=[WN], w3=[WN], r1=[R], rw=[ZC], r3=[R], rsend=[NB * H],
-                   rj1=[3 * R], rj2=[3 * R], l3=[3 * R], gg=[24 * R], pp=[NP * 3 * R], snd2=[NB * 6 * H],
+                   tsl=[72], cs=[72]))
+SCRATCH.update(_sb("uint16", shp16=[12], stg=[3, 7, 4], vl=[84], lb=[24], lc=[36], list2=[72], prm=[72], unperm=[72], rl=[72],
+                   ls=[576]))
+SCRATCH.update(_sb("float16", csg=[NB * H], colh=[12, 2, 16], q4=[4 * 128], sel=[2 * 128], c3=[72, 9], off=[72], idh=[128]))
+SCRATCH.update(_sb("bfloat16", vsend=[NB * 7 * H], eq=[576, 6], ones=[128], idb=[128], negb=[128], upb=[128], dnb=[128],
+                   idw=[6 * 128], al=[3 * R], nal=[3 * R], w1=[WN]))
+SCRATCH.update(_sb("float32", cw=[2 * ZC], csend=[2 * NB * H], pf=[8], sptf=[72], ext=[120],
+                   cl=[24, 16], cmpx=[96], nvf=[72], spf=[72], srt=[72], tmp=[72], tsf=[72], strd=[216], base=[72], ta=[72],
+                   istr=[72], bq=[72], fin=[576], rk2=[72], rk3=[72], gu=[72 * 16], tu=[72, 16],
+                   negf=[128], idf=[128], w2=[WN], w3=[WN], r1=[ZC], r2=[ZC], r3=[R], rsend=[NB * H],
+                   rj1=[2 * R], rj2=[2 * R], nl0=[R], l3=[3 * R], gg=[15 * R], pp=[NP * R], snd2=[NB * 6 * H],
                    snd3=[NB * 6 * H], yy=[10 * R]))
-SCRATCH["xl"] = ("psum", [128, 1536], "float32")
-for _i in range(5):
-    SCRATCH["a%d" % _i] = ("psum", [128, 512], "float32")
-ARR = ["c0", "v0", "r2"] + ["x%d%d" % (k, i) for k in (2, 3) for i in range(3)]
-SEMAPHORES = ["v", "s", "t", "g", "sent"] + ["a_" + a for a in ARR] + ["d%d" % i for i in range(16)]
+for _n in ("x1", "x2", "a0", "a1", "a2", "a4", "a5"):
+    SCRATCH[_n] = ("psum", [128, 512], "float32")
+SCRATCH["a3"] = ("psum", [128, 16, 32], "float32")
+NPIECE = len(CFG["cut"]) - 1
+ARR = ["c0", "v0", "r2"] + ["x%d%d" % (k, i) for k in (2, 3) for i in range(6)]
+SEMAPHORES = ["v", "s", "t", "g", "sent"] + ["a_" + a for a in ARR] + ["d%d" % i for i in range(24)]
 
 
 def rank_program(g, core, T, topo):
@@ -45,6 +57,7 @@ def rank_program(g, core, T, topo):
     cnt = {"v": 0, "s": 0, "t": 0, "g": 0, "sent": 0, "d": 0}
     clock = {q: {} for q in Q}
     writer, readers = {}, {}
+    npiece = len(CFG["cut"]) - 1
 
     def wait(q, tok):
         sem, n, clk = tok[0], tok[1], tok[2]
@@ -85,10 +98,10 @@ def rank_program(g, core, T, topo):
         call().then_inc(T.sem[q], 1)
         after((q, cnt[q], dict(clock[q]), q), rd, wr)
 
-    def mm(calls, rd, wr, each=False):
+    def mm(calls, rd, wr, each=False, start=True, stop=True):
         before("t", rd, wr, False)
         for i, (o, l, r) in enumerate(calls):
-            ins = g.tensor.matmul(o, l, r, each or i == 0, each or i == len(calls) - 1)
+            ins = g.tensor.matmul(o, l, r, each or (start and i == 0), each or (stop and i == len(calls) - 1))
         cnt["t"] += 1
         ins.then_inc(T.sem.t, 1)
         after(("t", cnt["t"], dict(clock["t"]), "t"), rd, wr)
@@ -109,7 +122,7 @@ def rank_program(g, core, T, topo):
             if not grp:
                 continue
             free = [e for e in topo.engines(src, grp[0]) if e not in used]
-            n = 4
+            n = CFG["eng"]
             while n * len(grp) > len(free):
                 n //= 2
             step = len(free) // n
@@ -121,6 +134,7 @@ def rank_program(g, core, T, topo):
     mine = plan(core)
     others = [p for p in range(N) if p != rank]
     arrive = sum(len(plan(T.cores[p])[core]) for p in others)
+    sent = []
 
     def send(name, src, width, dst, rd):
         before("g", rd, [], True)
@@ -134,6 +148,7 @@ def rank_program(g, core, T, topo):
                                         remote_sem=T.sem["a_" + name], src=src(b * width, (b + 1) * width), dst=dst(me)))
             cnt["sent"] += len(mine[c])
         g.remote_dma_fused(tr, local_sem=T.sem.sent)
+        sent.append(name)
 
     for a in ARR:
         writer["arr." + a] = ("a_" + a, arrive, {}, "far")
@@ -161,53 +176,72 @@ def rank_program(g, core, T, topo):
     def third(buf, t):
         return buf[:, 24 * t:24 * t + 24]
 
-    dma("y", T.shp[:], T.ship[:], [], ["shp"])
-    dma("s", T.colraw[1:128:2, :], T.col[:, 0:8 * R], [], ["colB"])
+    BANK = {n: T[n] for n in ("x1", "x2", "a0", "a1", "a2", "a3", "a4", "a5")}
+
+    def row(n):
+        return T.a3[:, 0:R // 32, :] if n == "a3" else BANK[n][:, 0:R]
+
     dma("y", T.colraw[0:128:2, :], T.col[:, 2 * R:10 * R], [], ["colA"])
-    dma("s", T.spt[:], T.spot[:], [], ["spt"])
+    dma("s", T.shp[:], T.ship[:], [], ["shp"])
+    dma("s", T.colraw[1:128:2, :], T.col[:, 0:8 * R], [], ["colB"])
+    dma("y", T.spt[:], T.spot[:], [], ["spt"])
     dma("y", T.w1[:, R:HB], T.val[:, 3 * R:10 * R], [], ["w1.own"])
     dma("y", T.al[:], T.val[:, 0:3 * R], [], ["al"])
 
-    op("g", lambda: g.iota(T.pi[:], [[0, 1]], 0, 1), [], ["pi"])
-    op("g", lambda: g.iota(T.nvi[:], [[0, 3], [16, 24]], 0, 1), [], ["nvi"])
     op("v", lambda: V.memset(T.ones[:], 1.0), [], ["ones"])
+    op("g", lambda: g.iota(T.pi[:], [[0, 1]], 0, 1), [], ["pi"])
     op("g", lambda: g.affine_select(T.idb[:], T.ones[:], [[-1, 128]], A.is_equal, 0.0, 0, 1), ["ones"], ["idb"])
-    op("v", lambda: V.memset(T.cw[:, ZC:ZC + 8], 0.0), [], ["cw.z"])
+    op("g", lambda: g.affine_select(T.upb[:], T.ones[:], [[-1, 128]], A.is_equal, 0.0, 16, 1), ["ones"], ["upb"])
+    op("g", lambda: g.affine_select(T.dnb[:], T.ones[:], [[-1, 128]], A.is_equal, 0.0, -16, 1), ["ones"], ["dnb"])
+    op("g", lambda: g.iota(T.nvi[:], [[0, 3], [16, 24]], 0, 1), [], ["nvi"])
     op("v", lambda: V.memset(T.w1[:, 0:R], 0.0), [], ["w1.z0"])
     for b in range(NB):
         op("v", lambda: V.memset(T.w1[:, HB + b * HS:HB + b * HS + H], 0.0), [], ["w1.z%d" % (b + 1)])
     ts(T.pt[:, 0:1], T.pi[:], 4, None, A.logical_shift_right, None, ["pi"], ["pt0"])
     ts(T.pt[:, 1:2], T.pi[:], 4, 1, A.logical_shift_right, A.bitwise_and, ["pi"], ["pt1"])
-    M0, M1, Z0, Z1, PH = [T.pf[:, i:i + 1] for i in range(5)]
+    M0, M1, PH = [T.pf[:, i:i + 1] for i in range(3)]
     ts(PH, T.pt[:, 0:1], 16.0, None, A.mult, None, ["pt0"], ["ph"])
     ts(M0, T.pt[:, 1:2], -1.0, 1.0, A.mult, A.add, ["pt1"], ["m0"])
     ts(M1, T.pt[:, 1:2], 1.0, None, A.mult, None, ["pt1"], ["m1"])
-    ts(Z0, T.pt[:, 1:2], float(ZC), None, A.mult, None, ["pt1"], ["z0"])
-    ts(Z1, T.pt[:, 1:2], -float(ZC), float(ZC), A.mult, A.add, ["pt1"], ["z1"])
-    ts(T.nvf[:], T.nvi[:], PH, 1.0 / R, A.subtract, A.mult, ["nvi", "ph"], ["nvf"])
     cp(T.idh[:], T.idb[:], ["idb"], ["idh"])
+
+    def move(e, f):
+        return T.q4[:, (2 * e + f) * 128:(2 * e + f + 1) * 128]
+
+    def both(e):
+        return T.sel[:, e * 128:(e + 1) * 128]
+
+    for e, f, src, key in ((0, 0, T.idb, "idb"), (1, 1, T.idb, "idb"), (0, 1, T.upb, "upb"), (1, 0, T.dnb, "dnb")):
+        ts(move(e, f), src[:], (M0, M1)[e], None, A.mult, None, [key, "m0", "m1"], ["q%d%d" % (e, f)])
+    for e in range(2):
+        tt(both(e), move(e, 0), move(e, 1), A.add, ["q%d0" % e, "q%d1" % e], ["sel%d" % e])
+    ts(T.nvf[:], T.nvi[:], PH, 1.0 / R, A.subtract, A.mult, ["nvi", "ph"], ["nvf"])
+    mv = ["q00", "q01", "q10", "q11"]
     act(T.idf[:], T.idb[:], ["idb"], ["idf"])
-    act(T.neg[:], T.idb[:], ["idb"], ["neg"], scale=-1.0)
+    act(T.negf[:], T.idb[:], ["idb"], ["negf"], scale=-1.0)
+    act(T.negb[:], T.idb[:], ["idb"], ["negb"], scale=-1.0)
     for w in range(6):
-        act(T.idw[:, w * 128:(w + 1) * 128], T.idb[:], ["idb"], ["idw%d" % w], scale=float(w + 2))
+        act(T.idw[:, w * 128:(w + 1) * 128], T.idb[:], ["idb"], ["idw%d" % w], scale=float(H * (w + 2)))
 
     col = ["colA", "colB"]
     cp(T.shp16[:], T.shp[:], ["shp"], ["shp16"])
-    cp(T.shpf[:], T.shp[:], ["shp"], ["shpf"])
+    cp(T.csg[:], T.colraw[:, 0:R].indirect(T.shp16[:, 0:12]), col + ["shp16"], ["csg"])
+    mm([(T.a0[:, e:2 * NB * H:2], both(e), T.csg[:]) for e in range(2)], ["csg", "sel0", "sel1"], ["Pa0"], True)
+    act(T.csend[:], T.a0[:, 0:2 * NB * H], ["Pa0"], ["csend"])
+    send("c0", lambda a, b: T.csend[:, a:b], 2 * H, lambda b: T.cw[:, 2 * (R + b * H):2 * (R + (b + 1) * H)], ["csend"])
+    cp(T.colh[:], T.colraw[:], col, ["colh"])
     cp(T.sptf[:], T.spt[:], ["spt"], ["sptf"])
-    cp(T.csend[:], T.colraw[:, 0:R].indirect(T.shp16[:, 0:12]), col + ["shp16"], ["csend"])
-    send("c0", lambda a, b: T.csend[:, a:b], H, lambda b: T.cw[:, R + b * H:R + (b + 1) * H], ["csend"])
+    for e in range(2):
+        mm([(T.a3[:, 0:12, 16 * e:16 * e + 16], move(e, f), T.colh[:, :, f, :]) for f in range(2)], mv + ["colh"], ["Pa3"])
+    for e in range(2):
+        mm([(row("a%d" % (1 + e)), both(e), T.colh[:])], ["colh", "sel%d" % e], ["Pa%d" % (1 + e)])
     stg = ["stg%d" % w for w in range(7)]
+    for w in range(7):
+        ts(T.stg[:, :, w, :], T.shp[:], float(w * R), None, A.add, None, ["shp"], [stg[w]])
+    cp(T.vl[:], T.stg[:], stg, ["vl"])
     for t in range(3):
         act(third(T.spf, t), third(T.sptf, t), ["sptf"], ["spf%d" % t], scale=1.0 / 1024, bias=3.0 + t / 4096.0)
-    for w in range(7):
-        act(T.stg[:, :, w, :], T.shpf[:], ["shpf"], [stg[w]], bias=float(w * R))
-
-    ts(T.in2[:, :, 0:16], T.colraw[:], M0, None, A.mult, None, col + ["m0"], ["in2a"])
-    ts(T.in2[:, :, 16:32], T.colraw[:], M1, None, A.mult, None, col + ["m1"], ["in2b"])
-    cp(T.cw[:, 0:R], T.colraw[:], col, ["cw.own"])
-    op("v", lambda: V.transpose(T.t2[:], T.in2[:]), ["in2a", "in2b"], ["t2"])
-    cp(T.vl[:], T.stg[:], stg, ["vl"])
+    op("v", lambda: V.transpose(T.cl[:], row("a3")), ["Pa3"], ["cl"])
     act(T.vsend[:], T.w1[:, R:HB].indirect(T.vl[:, 0:84]), ["w1.own", "vl"], ["vsend"])
     send("v0", lambda a, b: T.vsend[:, a:b], 7 * H, lambda b: T.w1[:, HB + b * HS + H:HB + (b + 1) * HS], ["vsend"])
     for k, W in ((2, T.w2), (3, T.w3)):
@@ -215,276 +249,338 @@ def rank_program(g, core, T, topo):
         for b in range(NB):
             op("g", lambda: g.iota(W[:, HB + b * HS:HB + b * HS + 2 * H], [[0, 2 * H]], 0, 0,
                                    allow_small_or_imprecise_dtypes=True), [], ["w%d.z%d" % (k, b + 1)])
-    for t in range(3):
-        tt(third(T.kk, t), T.t2[:, :, 2 * t + 1], T.t2[:, :, 2 * t + 17], A.add, ["t2"], ["kk%d" % t])
-    tt(T.c3[:, 0:24, 0:7], T.t2[:, :, 2:16:2], T.t2[:, :, 18:32:2], A.add, ["t2"], ["c30"])
-    tt(T.ext[:, 24:96], T.kk[:], T.spf[:], A.add, ["kk0", "kk1", "kk2", "spf0", "spf1", "spf2"], ["key"])
+    for e in range(2):
+        act(T.cw[:, e:2 * R:2], row("a%d" % (1 + e)), ["Pa%d" % (1 + e)], ["cw%d" % e])
+
     k0, k1, k2 = [third(T.ext, t + 1) for t in range(3)]
     s0, s1, s2 = [third(T.srt, t) for t in range(3)]
     m0, m1, m2 = [third(T.tmp, t) for t in range(3)]
-    tt(m1, k0, k1, A.max, ["key"], ["tm1"])
-    tt(m0, k0, k1, A.min, ["key"], ["tm0"])
-    tt(m2, m1, k2, A.min, ["tm1", "key"], ["tm2"])
-    tt(s0, m0, k2, A.min, ["tm0", "key"], ["s0"])
-    tt(s2, m1, k2, A.max, ["tm1", "key"], ["s2"])
+    for t in range(3):
+        tt(third(T.ext, t + 1), T.cl[:, :, 2 * t + 1], third(T.spf, t), A.add, ["cl", "spf%d" % t], ["k%d" % t])
+    key = ["k0", "k1", "k2"]
+    tt(m1, k0, k1, A.max, key[0:2], ["tm1"])
+    tt(m0, k0, k1, A.min, key[0:2], ["tm0"])
+    tt(m2, m1, k2, A.min, ["tm1", "k2"], ["tm2"])
+    tt(s0, m0, k2, A.min, ["tm0", "k2"], ["s0"])
+    tt(s2, m1, k2, A.max, ["tm1", "k2"], ["s2"])
     tt(s1, m0, m2, A.max, ["tm0", "tm2"], ["s1"])
+    cp(T.c3[:, 0:24, 0:7], T.cl[:, :, 2:16:2], ["cl"], ["c30"])
     ts(T.ki[:], T.srt[:], 4096.0, None, A.mult, None, ["s0", "s1", "s2"], ["ki"])
+    cp(T.c3[:, 24:48, 0:7], T.cl[:, :, 2:16:2], ["cl"], ["c31"])
     ts(T.sps[:], T.ki[:], 2, 1023, A.logical_shift_right, A.bitwise_and, ["ki"], ["sps"])
-    ts(T.cs[:], T.ki[:], 12, None, A.logical_shift_right, None, ["ki"], ["cs"])
-    ts(T.list2[:, 0:144:2], T.sps[:], M0, Z0, A.mult, A.add, ["sps", "m0", "z0"], ["l2a"])
-    ts(T.list2[:, 1:144:2], T.sps[:], M1, Z1, A.mult, A.add, ["sps", "m1", "z1"], ["l2b"])
-
-    cwk = ["cw.own", "cw.z", "arr.c0", "l2a", "l2b"]
-    for j in range(3):
-        act(T.gu[:, 768 * j:768 * j + 768], T.cw[:, 0:ZC + 8].indirect(T.list2[:, 48 * j:48 * j + 48]), cwk, ["gu%d" % j])
-    ts(T.c3[:, 0:24, 7], third(T.cs, 1), -3.0, None, A.add, None, ["cs"], ["c31"])
-    ts(T.c3[:, 0:24, 8], third(T.cs, 2), -3.0, None, A.add, None, ["cs"], ["c32"])
-    ts(T.ts[:], T.ki[:], 3, None, A.bitwise_and, None, ["ki"], ["ts"])
+    ts(T.tsl[:], T.ki[:], 3, None, A.bitwise_and, None, ["ki"], ["tsl"])
+    ts(T.off[:], T.sps[:], 2.0, M1, A.mult, A.add, ["sps", "m1"], ["off"])
+    cp(T.c3[:, 48:72, 0:7], T.cl[:, :, 2:16:2], ["cl"], ["c32"])
+    for e in range(2):
+        mm([(T.a4[:, e:72:2], move(e, f), T.off[:, f:72:2]) for f in range(2)], mv + ["off"], ["Pa4"])
+    tt(T.tsf[:], T.tsl[:], T.nvf[:], A.add, ["tsl", "nvf"], ["tsf"])
     ts(T.blk[:], T.ki[:], 8, 15, A.logical_shift_right, A.bitwise_and, ["ki"], ["blk"])
-    cr = ["c30", "c31", "c32"]
-    cp(T.c3[:, 24:48, :], T.c3[:, 0:24, :], cr, ["c33"])
-    cp(T.c3[:, 48:72, :], T.c3[:, 0:24, :], cr, ["c34"])
-    cr += ["c33", "c34"]
-    tt(T.tsf[:], T.ts[:], T.nvf[:], A.add, ["ts", "nvf"], ["tsf"])
-    ts(T.ta[:], T.blk[:], 6.0, float(HS - H), A.is_ge, A.mult, ["blk"], ["ta"])
-    ts(T.tb[:], T.blk[:], 6.0, float(H - R), A.is_ge, A.mult, ["blk"], ["tb"])
     ts(T.prm[:], T.tsf[:], float(R), 0.25, A.mult, A.add, ["tsf"], ["prm"])
-    act(T.als[:], T.al[:, 0:3 * R].indirect(T.prm[:, 0:72]), ["al", "prm"], ["als"])
-    act(T.r1[:], T.w1[:, R:2 * R], ["w1.own"], ["r1"], scale=-1.0, bias=2.0)
-    act(T.ext[:, 0:24], k2, ["key"], ["ext0"])
-    act(T.ext[:, 96:120], k0, ["key"], ["ext1"])
-    tt(T.ta[:], T.ta[:], T.blk[:], A.mult, ["ta", "blk"], ["ta"])
-    ts(T.strd[:], T.tb[:], float(R), None, A.add, None, ["tb"], ["strd"])
-    ts(T.istr[:], T.tb[:], (1.0 / H - 1.0 / R) / (H - R), 1.0 / R, A.mult, A.add, ["tb"], ["istr"])
-    tt(T.base[:], T.ta[:], T.sps[:], A.add, ["ta", "sps"], ["base"])
-    cp(T.lb[:], T.stg[:, :, 0:2, :], stg, ["lb"])
-    tt(T.bq[:], T.base[:], T.istr[:], A.mult, ["base", "istr"], ["bq"])
-    cp(T.rl2[:], T.sps[:], ["sps"], ["rl2"])
+    cp(T.list2[:], T.a4[:, 0:72], ["Pa4"], ["list2"])
+    act(T.nal[:], T.al[:, 0:3 * R].indirect(T.prm[:, 0:72]), ["al", "prm"], ["nal"], scale=-1.0)
 
-    ACC = [T.a0, T.a1, T.a2, T.a3, T.a4]
-
-    def cbank(i):
-        return (T.xl, 512 * i, "Pxl") if i < 3 else (ACC[(0, 1, 4)[i % 3]], 0, "Pa%d" % (0, 1, 4)[i % 3])
+    JOINS = [3] * 7 + [2, 1]
+    LIST = [72 * i for i in range(8)] + [552]
+    CB = [("x1", 0), ("x2", 0), ("a0", 0), ("a1", 0), ("a2", 0), ("a4", 0), ("a5", 0), ("a0", 0), ("a0", 288)]
 
     def spread(i):
         s = (i + 1 if i < 6 else 0) if i < 7 else 15 - i
-        n = 72 if i < 7 else 24 * (9 - i)
-        B, o, bk = cbank(i)
-        mm([(B[:, o + w:o + 6 * n:6], T.idh[:], T.c3[:, 0:n, s]) for w in range(6)], cr + ["idh"], [bk], True)
+        n = 24 * JOINS[i]
+        bk, o = CB[i]
+        mm([(BANK[bk][:, o + w:o + 6 * n:6], T.idh[:], T.c3[:, 0:n, s]) for w in range(6)],
+           (["c30", "c31", "c32"] if i < 7 else ["c3a", "c3b", "c3c"]) + ["idh"], ["P" + bk], True)
 
     for i in range(6):
         spread(i)
+    ts(T.ta[:], T.blk[:], 6.0, float(HS - H), A.is_ge, A.mult, ["blk"], ["ta"])
+    ts(T.cs[:], T.ki[:], 12, None, A.logical_shift_right, None, ["ki"], ["cs"])
+    tt(T.ta[:], T.ta[:], T.blk[:], A.mult, ["ta", "blk"], ["ta"])
+    ts(T.istr[:], T.blk[:], 6.0, H / R, A.is_ge, A.max, ["blk"], ["istr"])
+    ts(T.strd[:, 0:72], T.blk[:], 6.0, H / R, A.is_lt, A.max, ["blk"], ["strd"])
+    tt(T.base[:], T.ta[:], T.sps[:], A.add, ["ta", "sps"], ["base"])
+    cp(T.lb[:], T.stg[:, :, 0:2, :], stg, ["lb"])
+    tt(T.bq[:], T.base[:], T.istr[:], A.mult, ["base", "istr"], ["bq"])
+    cp(T.lc[:], T.stg[:, :, 0:3, :], stg, ["lc"])
+    cp(T.rl[:], T.sps[:], ["sps"], ["rl"])
+    for o, n in ((72, 72), (144, 48), (192, 24)):
+        cp(T.strd[:, o:o + n], T.strd[:, 0:n], ["strd"], ["strd%d" % o])
+    strd = ["strd", "strd72", "strd144", "strd192"]
+    ts(T.c3[:, 0:24, 7], third(T.cs, 1), -3.0, None, A.add, None, ["cs"], ["c3a"])
+    ts(T.c3[:, 0:24, 8], third(T.cs, 2), -3.0, None, A.add, None, ["cs"], ["c3b"])
+    ts(T.c3[:, 24:48, 8], third(T.cs, 2), -3.0, None, A.add, None, ["cs"], ["c3c"])
+    cp(T.ext[:, 0:24], k2, ["k2"], ["ext0"])
+    cp(T.ext[:, 96:120], k0, ["k0"], ["ext1"])
+    tt(T.cmpx[:], T.ext[:, 0:96], T.ext[:, 24:120], A.is_gt, key + ["ext0", "ext1"], ["cmpx"])
+    tt(T.rk2[:], T.cmpx[:, 24:96], T.cmpx[:, 0:72], A.subtract, ["cmpx"], ["rk2"])
+    tt(T.rk3[:], T.rk2[:], T.nvf[:], A.add, ["rk2", "nvf"], ["rk3"])
+    ts(T.unperm[:], T.rk3[:], float(R), R + 0.25, A.mult, A.add, ["rk3"], ["unperm"])
+
+    cwk = ["cw0", "cw1", "arr.c0", "list2"]
     for j in range(3):
-        op("v", lambda: V.transpose(T.tu[:, 24 * j:24 * j + 24, :], T.gu[:, 768 * j:768 * j + 768]), ["gu%d" % j], ["tu%d" % j])
-        if j == 0:
-            tt(T.rl[:], T.base[:], T.strd[:], A.add, ["base", "strd"], ["rl"])
-        for i in ((), (0,), (1, 2))[j]:
-            tt(T.upc[:, 144 * i:144 * i + 144], T.tu[:, 24 * i:24 * i + 24, 4:16:2], T.tu[:, 24 * i:24 * i + 24, 20:32:2],
-               A.add, ["tu%d" % i], ["upc%d" % i])
-    cp(T.rl1[:], T.rl[:], ["rl"], ["rl1"])
+        (act if j else cp)(T.gu[:, R * j:R * j + R], T.cw[:, 0:2 * ZC].indirect(third(T.list2, j)), cwk, ["gu%d" % j])
+    for j in range(3):
+        op("v", lambda: V.transpose(T.tu[:, 24 * j:24 * j + 24, :], T.gu[:, R * j:R * j + R]), ["gu%d" % j], ["tu%d" % j])
 
     def compare(i):
-        n = 72 if i < 7 else 24 * (9 - i)
-        o = 72 * i if i < 8 else 552
-        B, c, bk = cbank(i)
-        tt(T.eq[:, o:o + n, :], B[:, c:c + 6 * n], T.upc[:, 0:6 * n], A.is_equal, [bk, "upc0", "upc1", "upc2"], ["eq%d" % i])
+        n = 24 * JOINS[i]
+        bk, o = CB[i]
+        tt(T.eq[:, LIST[i]:LIST[i] + n, :], BANK[bk][:, o:o + 6 * n], T.tu[:, 0:n, 4:16:2], A.is_equal,
+           ["P" + bk, "tu0", "tu1", "tu2"], ["eq%d" % i])
 
-    PARTS = [((0, 72), (72, 72))] * 3 + [((0, 72), (72, 48), (120, 24))]
+    GROUP = [(0, 1), (2, 3), (4, 5), (6, 7, 8)]
+    WB = ["a5", "a0", "a2", "a1"]
 
     def weigh(lg):
-        B = ACC[2 + lg % 2]
-        e = ["eq%d" % i for i in ((2 * lg, 2 * lg + 1) if lg < 3 else (6, 7, 8))]
+        B = BANK[WB[lg]]
         calls = [(B[:, 0:144], T.idw[:, w * 128:(w + 1) * 128], T.eq[:, 144 * lg:144 * lg + 144, w]) for w in range(6)]
-        calls += [(B[:, o:o + n], T.idf[:], T.bq[:, 0:n]) for o, n in PARTS[lg]]
-        mm(calls, e + ["idw%d" % w for w in range(6)] + ["idf", "bq"], ["Pa%d" % (2 + lg % 2)])
+        calls += [(B[:, LIST[i] - 144 * lg:LIST[i] - 144 * lg + 24 * JOINS[i]], T.idf[:], T.bq[:, 0:24 * JOINS[i]]) for i in GROUP[lg]]
+        mm(calls, ["eq%d" % i for i in GROUP[lg]] + ["idw%d" % w for w in range(6)] + ["idf", "bq"], ["P" + WB[lg]])
 
     def final(lg, step):
+        c = slice(144 * lg, 144 * lg + 144)
         if step == 0:
-            for o, n in PARTS[lg]:
-                tt(T.fin[:, 144 * lg + o:144 * lg + o + n], ACC[2 + lg % 2][:, o:o + n], T.strd[:, 0:n], A.mult,
-                   ["Pa%d" % (2 + lg % 2), "strd"], ["fin%d.%d" % (lg, o)])
+            o = 72 if lg == 3 else 0
+            tt(T.fin[:, c], BANK[WB[lg]][:, 0:144], T.strd[:, o:o + 144], A.mult, ["P" + WB[lg]] + strd, ["fin%d" % lg])
         else:
-            ts(T.ls[:, 144 * lg:144 * lg + 144], T.fin[:, 144 * lg:144 * lg + 144], 0.25, None, A.add, None,
-               ["fin%d.%d" % (lg, o) for o, n in PARTS[lg]], ["ls%d" % lg])
+            ts(T.ls[:, c], T.fin[:, c], float(R // H), 0.25, A.mult, A.add, ["fin%d" % lg], ["ls%d" % lg])
 
     WIN = {1: T.w1, 2: T.w2, 3: T.w3}
     WK = {1: ["w1.own", "arr.v0"] + ["w1.z%d" % i for i in range(4)]}
     for k in (2, 3):
         WK[k] = (["w%d.u%d" % (k, w) for w in range(6)] + ["w%d.z%d" % (k, i) for i in range(4)]
-                 + ["arr.x%d%d" % (k, i) for i in range(3)])
-    ITEM = [(3 * i, 3) for i in range(7)] + [(21, 2), (23, 1)]
-    st = {"p": 0, "a": 0, "keep": None}
-    held = {}
+                 + ["arr.x%d%d" % (k, i) for i in range(npiece)])
+    NL0 = {1: (T.nal[:, 0:R], "nal"), 2: (T.nal[:, 0:R], "nal"), 3: (T.nl0[:], "nl0")}
+    BANKS = {1: "a3 a5 a0 a1 a4 a2 a5 a3 x1".split(), 2: "a4 a2 a0 a1 a3 a4 a1 a0 a2".split(),
+             3: "a2 a0 a5 a4 a3 a1 a3 a4 a5".split()}
+    st = {"p": 0}
+    prods = {}
 
-    def gather(k, i, q="s", j0=0, j1=3):
-        o, n = ITEM[i]
-        j1 = min(j1, n)
-        (act if q == "s" else cp)(T.gg[:, (o + j0) * R:(o + j1) * R],
-                                  WIN[k][:, 0:WN].indirect(T.ls[:, 24 * (o + j0):24 * (o + j1)]),
-                                  WK[k] + ["ls%d" % min(i // 2, 3)], ["g%d" % (o + j) for j in range(j0, j1)])
+    def window(k, i, j0, j1):
+        return (WIN[k][:, 0:WN].indirect(T.ls[:, LIST[i] + 24 * j0:LIST[i] + 24 * j1]), WK[k] + ["ls%d" % min(i // 2, 3)])
 
-    def aval(i):
-        if i < 6:
-            return T.w1[:, (2 + i) * R:(3 + i) * R]
-        if i == 6:
-            return T.w1[:, R:2 * R]
-        return T.als[:, (9 - i) * R:(10 - i) * R]
-
-    def prod(p, j0, j1):
-        return T.pp[:, (p * 3 + j0) * R:(p * 3 + j1) * R]
-
-    def accumulate(i, npe):
-        if st["a"] % 5 == st["keep"]:
-            st["a"] += 1
-        a = st["a"] % 5
-        st["a"] += 1
-        calls = [(ACC[a][:, 0:R], T.idb[:], aval(i))]
-        rd = ["idb", "neg", "als", "w1.own"]
-        if not npe:
-            held[i] = [None, None, 0]
-        for j in range(npe):
-            calls.append((ACC[a][:, 0:R], T.neg[:], prod(held[i][0], j, j + 1)))
-            rd.append("p%d.%d" % (held[i][0], j))
-        mm(calls, rd, ["Pa%d" % a])
-        held[i][1] = a
-
-    def mult(i, npe, cut=False):
-        o, n = ITEM[i]
+    def newprod(i, j):
         p = st["p"] % NP
         st["p"] += 1
-        held[i] = [p, held[i][1] if npe is None else None, npe or 0]
-        for j0, j1 in (((0, npe), (npe, n)) if cut else ((0, n),)):
-            tt(prod(p, j0, j1), T.gg[:, (o + j0) * R:(o + j1) * R], T.xl[:, j0 * R:j1 * R], A.mult,
-               ["g%d" % (o + j) for j in range(j0, j1)] + ["Pxl"], ["p%d.%d" % (p, j) for j in range(j0, j1)])
-            if j0 == 0 and npe:
-                accumulate(i, npe)
+        prods[i, j] = (T.pp[:, p * R:(p + 1) * R], "p%d" % p)
+        return prods[i, j]
 
-    def lessen(i):
-        p, a, j = held[i]
-        tt(ACC[a][:, 0:R], ACC[a][:, 0:R], prod(p, j, j + 1), A.subtract, ["Pa%d" % a, "p%d.%d" % (p, j)], ["Pa%d" % a])
-        held[i][2] = j + 1
+    def got(i, j):
+        return T.gg[:, (2 * i + j - 1) * R:(2 * i + j) * R], "g%d" % i
 
-    def evict(i, out, key):
-        p, a, j = held[i]
-        tt(out, ACC[a][:, 0:R], prod(p, j, j + 1), A.subtract, ["Pa%d" % a, "p%d.%d" % (p, j)], [key])
+    def gather(k, i):
+        src, rd = window(k, i, 1, JOINS[i])
+        act(T.gg[:, 2 * i * R:(2 * i + JOINS[i] - 1) * R], src, rd, ["g%d" % i])
 
-    def scale(i, rj, rk, out, ok):
-        a = held[i][1]
-        j = 9 - i
-        tt(out[:, j * R:(j + 1) * R], ACC[a][:, 0:R], rj[:, j * R:(j + 1) * R], A.mult, ["Pa%d" % a, rk], [ok])
+    def fused(k, i):
+        src, rd = window(k, i, 0, 1)
+        p, pk = newprod(i, 0)
+        tt(p, src, NL0[k][0], A.mult, rd + [NL0[k][1]], [pk])
+
+    def opened(k, i):
+        b = BANKS[k][i]
+        mm([(row(b), T.idb[:], T.w1[:, 0:R])], ["idb", "w1.z0"], ["P" + b], stop=False)
+
+    def direct(k, i):
+        b = BANKS[k][i]
+        u, uk = got(i, 1)
+        tt(row(b), u, row("x1"), A.mult, [uk, "Px1"], ["P" + b])
+
+    def second(k, i):
+        u, uk = got(i, 2)
+        p, pk = newprod(i, 2)
+        tt(p, u, row("x2"), A.mult, [uk, "Px2"], [pk])
+
+    def total(k, i, js):
+        b = BANKS[k][i]
+        if i < 7:
+            c = (2 + i) * R if i < 6 else R
+            calls = [(row(b), T.idb[:], T.w1[:, c:c + R])]
+        else:
+            calls = [(row(b), T.idb[:] if b == "x1" else T.negb[:], T.nal[:, (9 - i) * R:(10 - i) * R])]
+        calls += [(row(b), T.negf[:] if b == "x1" else T.idf[:], prods[i, j][0]) for j in js]
+        mm(calls, ["idb", "negb", "idf", "negf", "nal", "w1.own"] + [prods[i, j][1] for j in js] + ([] if i == 8 else ["P" + b]),
+           ["P" + b], start=(i == 8))
+
+    def evict(k, i, out, key):
+        b = BANKS[k][i]
+        if CFG["out"][k][i] == "s":
+            act(out, row(b), ["P" + b], [key])
+        else:
+            tt(out, row(b), prods[i, 2][0], A.add, ["P" + b, prods[i, 2][1]], [key])
+
+    def scale(k, i, rj, rk, out, ok):
+        b = BANKS[k][i]
+        tt(out, row(b), rj[:, (8 - i) * R:(9 - i) * R], A.mult, ["P" + b, rk], [ok])
+
+    def later(f, *a):
+        return lambda: f(*a)
 
     def ship(k, c, q):
         SB = T.snd2 if k == 2 else T.snd3
-        w0, o = 2 * c, NB * 2 * c * H
-        src = WIN[k][:, (2 + w0) * R:(4 + w0) * R].indirect(T.lb[:, 0:24])
+        w0, w1 = CFG["cut"][c], CFG["cut"][c + 1]
+        n, o = w1 - w0, NB * w0 * H
+        src = WIN[k][:, (2 + w0) * R:(2 + w1) * R].indirect((T.shp16, T.lb, T.lc)[n - 1][:, 0:12 * n])
         key = "snd%d%d" % (k, c)
-        (act if q == "s" else cp)(SB[:, o:o + NB * 2 * H], src, ["w%d.u%d" % (k, w0), "w%d.u%d" % (k, w0 + 1), "lb"], [key])
-        send("x%d%d" % (k, c), lambda a, b: SB[:, o + a:o + b], 2 * H,
-             lambda b: WIN[k][:, HB + b * HS + (2 + w0) * H:HB + b * HS + (4 + w0) * H], [key])
+        (act if q == "s" else cp)(SB[:, o:o + NB * n * H], src, ["w%d.u%d" % (k, w) for w in range(w0, w1)] + ["shp16", "lb", "lc"], [key])
+        send("x%d%d" % (k, c), lambda a, b: SB[:, o + a:o + b], n * H,
+             lambda b: WIN[k][:, HB + b * HS + (2 + w0) * H:HB + b * HS + (2 + w1) * H], [key])
 
-    def newton(step, r=None, rk=None, out=None, ok=None):
-        a = st["keep"]
-        P, pk = ACC[a][:, 0:R], "Pa%d" % a
+    def ships(k):
+        return {("E", CFG["cut"][c + 1] - 1): [later(ship, k, c, CFG["shipq"][c])] for c in range(npiece)}
+
+    def newton(k, step, r, rk, out=None, ok=None):
+        b = BANKS[k][6]
+        P, pk = row(b), "P" + b
         if step == 0:
             tt(P, P, r, A.mult, [pk, rk], [pk])
         elif step == 1:
             act(P, P, [pk], [pk], scale=-1.0, bias=2.0)
         else:
             tt(out, P, r, A.mult, [pk, rk], [ok])
-            st["keep"] = None
 
-    def uppers(k, mid, done, dst):
-        npe = NPE[k]
-        for w in range(7):
-            if w < 6:
-                mult(w, npe[w], npe[w] == 1 or w == 5)
-                if w in mid:
-                    mid[w]()
-            if w:
-                for _ in range(2 - npe[w - 1]):
-                    lessen(w - 1)
-                evict(w - 1, *dst(w - 1))
-                if w - 1 in done:
-                    done[w - 1]()
+    def items(k, order, dst, extra, lag):
+        def late(i):
+            return JOINS[i] < 3 or CFG["out"][k][i] == "v"
+
+        def stage(x, i):
+            if x == "F":
+                fused(k, i)
+                if JOINS[i] == 1:
+                    total(k, i, [0])
+            elif x == "E":
+                if dst(i):
+                    evict(k, i, *dst(i))
+            elif x == "S":
+                if JOINS[i] == 3:
+                    second(k, i)
+                    if not late(i):
+                        total(k, i, [0, 2])
+            elif JOINS[i] > 1:
+                if x == "G":
+                    gather(k, i)
+                else:
+                    direct(k, i)
+                    if late(i):
+                        total(k, i, [0])
+
+        for m in range(len(order) + max(lag.values())):
+            for x in lag:
+                if 0 <= m - lag[x] < len(order):
+                    i = order[m - lag[x]]
+                    stage(x, i)
+                    for f in extra.get((x, i), ()):
+                        f()
 
     def up(k):
         return lambda w: (WIN[k][:, (2 + w) * R:(3 + w) * R], "w%d.u%d" % (k, w))
 
-    compare(0); compare(1); weigh(0)
-    compare(2); compare(3); weigh(1); spread(6); final(0, 0); compare(4); spread(7); final(0, 1)
-    gather(1, 0); gather(1, 1)
-    compare(5); weigh(2); spread(8); final(1, 0); compare(6); final(1, 1)
-    gather(1, 2); gather(1, 3)
-    for o, n in ((0, 512), (512, 512), (1024, 128)):
-        mm([(T.xl[:, o:o + n], T.idb[:], T.als[:, o:o + n])], ["idb", "als"], ["Pxl"])
-    final(2, 0); compare(7); final(2, 1); compare(8); weigh(3)
-    gather(1, 4)
-    uppers(1, {0: lambda: final(3, 0), 1: lambda: final(3, 1)},
-           {1: lambda: (ship(2, 0, "s"), gather(1, 5), gather(1, 8), gather(1, 7)),
-            3: lambda: (ship(2, 1, "s"), gather(1, 6)),
-            5: lambda: ship(2, 2, "v")}, up(2))
-    act(T.rj1[:], T.w1[:, 0:WN].indirect(T.rl1[:, 0:72]), WK[1] + ["rl1"], ["rj1"], scale=-1.0, bias=2.0)
-    accumulate(8, 0); mult(7, 1); mult(8, None); mult(6, 3)
-    st["keep"] = held[6][1]
-    tt(T.cmpx[:], T.ext[:, 0:96], T.ext[:, 24:120], A.is_gt, ["key", "ext0", "ext1"], ["cmpx"])
-    evict(8, T.xl[:, R:2 * R], "Pxl")
-    tt(T.rk2[:], T.cmpx[:, 24:96], T.cmpx[:, 0:72], A.subtract, ["cmpx"], ["rk2"])
-    evict(7, T.xl[:, 2 * R:3 * R], "Pxl")
-    tt(T.rk3[:], T.rk2[:], T.nvf[:], A.add, ["rk2", "nvf"], ["rk3"])
-    ts(T.unperm[:], T.rk3[:], float(R), R + 0.25, A.mult, A.add, ["rk3"], ["unperm"])
-    newton(0, T.r1[:], "r1")
-    newton(1)
+    def merged(*ds):
+        out = {}
+        for d in ds:
+            for x in d:
+                out.setdefault(x, []).extend(d[x])
+        return out
 
-    gather(2, 0, "v")
-    for i in range(1, 5):
-        gather(2, i)
+    def opens(k, *pairs):
+        return {("E", e): [later(opened, k, i)] for e, i in pairs}
+
+    def rtable():
+        act(T.r1[:, 0:R], T.w1[:, R:2 * R], ["w1.own"], ["r1.own"], scale=-1.0, bias=2.0)
+        for b in range(NB):
+            c = HB + b * HS + H
+            act(T.r1[:, R + b * H:R + (b + 1) * H], T.w1[:, c:c + H], ["arr.v0"], ["r1.%d" % b], scale=-1.0, bias=2.0)
+
+    R1 = ["r1.own", "r1.0", "r1.1", "r1.2", "rl"]
+    R2 = ["r2.own", "arr.r2", "rl"]
+
+    def minus_r(out, key, tab, rd):
+        act(out[:], tab[:, 0:ZC].indirect(T.rl[:, 24:72]), rd, [key], scale=-1.0)
+
+    def lowest(out, key, tab, rd):
+        tt(out, tab[:, 0:ZC].indirect(T.rl[:, 0:24]), T.nal[:, 0:R], A.mult, rd + ["nal"], [key])
 
     def rsend():
-        act(T.rsend[:], T.rw[:, 0:R].indirect(T.shp16[:, 0:12]), ["rw.own", "shp16"], ["rsend"])
-        send("r2", lambda a, b: T.rsend[:, a:b], H, lambda b: T.rw[:, R + b * H:R + (b + 1) * H], ["rsend"])
+        act(T.rsend[:], T.r2[:, 0:R].indirect(T.shp16[:, 0:12]), ["r2.own", "shp16"], ["rsend"])
+        send("r2", lambda a, b: T.rsend[:, a:b], H, lambda b: T.r2[:, R + b * H:R + (b + 1) * H], ["rsend"])
 
-    uppers(2, {1: lambda: newton(2, T.r1[:], "r1", T.rw[:, 0:R], "rw.own")},
-           {1: lambda: (ship(3, 0, "s"), gather(2, 5), rsend()),
-            3: lambda: (ship(3, 1, "s"), gather(2, 8), gather(2, 7), gather(2, 6)),
-            5: lambda: ship(3, 2, "v")}, up(3))
-    act(T.rj2[:], T.rw[:, 0:ZC].indirect(T.rl2[:, 0:72]), ["rw.own", "arr.r2", "rl2"], ["rj2"])
-    accumulate(9, 0)
-    mult(8, 1); mult(7, 2); mult(6, 3)
-    st["keep"] = held[6][1]
-    scale(9, T.rj2, "rj2", T.l3, "l30")
-    scale(9, T.rj1, "rj1", T.xl, "Pxl")
-    scale(8, T.rj1, "rj1", T.xl, "Pxl")
-    scale(7, T.rj1, "rj1", T.xl, "Pxl")
+    upper, rest = [0, 1, 2, 3, 4, 5], [8, 7, 6]
+    compare(0); compare(1); weigh(0)
+    for j in (1, 2):
+        mm([(row("x%d" % j), T.idb[:], T.nal[:, j * R:(j + 1) * R])], ["idb", "nal"], ["Px%d" % j])
+    rtable()
+    compare(2); final(0, 0); compare(3); weigh(1); final(0, 1)
+    opened(1, 0); opened(1, 1)
+    items(1, upper, up(2), merged(ships(2), {
+        ("F", 0): [later(compare, 4), later(final, 1, 0), later(opened, 1, 2), later(opened, 1, 3)],
+        ("F", 1): [later(compare, 5), later(weigh, 2), later(final, 1, 1), later(opened, 1, 4)],
+        ("D", 0): [later(final, 2, 0), later(opened, 1, 5)],
+        ("S", 0): [later(final, 2, 1)],
+        ("E", 1): [later(spread, 6)],
+        ("E", 2): [later(spread, 7), later(spread, 8)],
+    }, opens(1, (0, 7)), opens(2, (4, 0), (5, 1))), CFG["lag1"])
+    minus_r(T.rj1, "rj1", T.r1, R1)
+    compare(6); compare(7); compare(8); weigh(3)
+    opened(1, 6); opened(2, 2)
+    lowest(T.nl0[:], "nl0", T.r1, R1)
+    final(3, 0)
+    opened(2, 3)
+    final(3, 1)
+    gather(1, 7); gather(1, 6)
+    fused(1, 7); fused(1, 6); direct(1, 7); total(1, 7, [0]); fused(1, 8); direct(1, 6); second(1, 6)
+    total(1, 8, [0])
+    act(row("x2"), row(BANKS[1][7]), ["P" + BANKS[1][7]], ["Px2"], scale=-1.0)
+    total(1, 6, [0, 2])
+    opened(2, 4)
+
+    r1own, r2own = (T.r1[:, 0:R], "r1.own"), (T.r2[:, 0:R], "r2.own")
+
+    def step_r():
+        newton(1, 0, *r1own); newton(1, 1, None, None)
+
+    def send_r():
+        newton(1, 2, *r1own, *r2own); rsend()
+
+    nw = CFG["newton"]
+    items(2, upper, up(3), merged(ships(3), opens(2, (0, 5), (2, 7), (3, 6)), opens(3, (4, 6), (5, 7)),
+                                  {nw[0]: [step_r], nw[1]: [send_r]}), CFG["lag2"])
+    gather(2, 7); gather(2, 6)
+    fused(2, 8); total(2, 8, [0]); fused(2, 7); direct(2, 7); total(2, 7, [0])
+    minus_r(T.rj2, "rj2", T.r2, R2)
+    fused(2, 6); direct(2, 6); second(2, 6); total(2, 6, [0, 2])
+    scale(2, 8, T.rj1, "rj1", row("x1"), "Px1")
+    opened(3, 0)
+    scale(2, 7, T.rj1, "rj1", row("x2"), "Px2")
+    opened(3, 1)
+    lowest(T.l3[:, 0:R], "l30", T.r2, R2)
+    newton(2, 0, *r2own)
+    newton(2, 1, None, None)
 
     def out(c0, c1, keys):
         dma("y", T.y[:, c0:c1], T.yy[:, c0:c1], keys, ["y%d" % c0])
 
-    def ys(s):
-        return T.yy[:, s * R:(s + 1) * R], "yy%d" % s
+    def ys(i):
+        s = 4 + i if i < 6 else 3
+        return (T.yy[:, s * R:(s + 1) * R], "yy%d" % s) if i < 7 else None
 
-    gather(3, 7); gather(3, 6, "s", 1, 3)
-    gather(3, 8, "v"); gather(3, 6, "v", 0, 1)
-    mult(8, 1)
-    newton(0, T.rw[:, 0:R], "rw.own")
-    newton(1)
-    for i in (0, 1, 2, 3):
-        gather(3, i)
-    mult(7, 2)
-    scale(8, T.rj2, "rj2", T.l3, "l31")
-    mult(6, 2)
-    newton(2, T.rw[:, 0:R], "rw.own", T.r3[:], "r3")
-    dma("y", T.inv[:], T.r3[:], ["r3"], ["inv"])
-    scale(7, T.rj2, "rj2", T.l3, "l32")
-    act(T.yy[:, 0:3 * R], T.l3[:, 0:3 * R].indirect(T.unperm[:, 0:72]), ["l30", "l31", "l32", "unperm"], ["yyl"])
-    gather(3, 4)
-    gather(3, 5, "s", 0, 1); gather(3, 5, "s", 1, 3)
-    done = {w: (lambda w=w: out((4 + w) * R, (5 + w) * R, ["yy%d" % (4 + w)])) for w in range(6)}
-    uppers(3, {0: lambda: (evict(6, *ys(3)), out(3 * R, 4 * R, ["yy3"])), 4: lambda: out(0, 3 * R, ["yyl"])},
-           done, lambda w: ys(4 + w))
+    def lower():
+        act(T.yy[:, 0:3 * R], T.l3[:, 0:3 * R].indirect(T.unperm[:, 0:72]), ["l30", "l31", "l32", "unperm"], ["yyl"], scale=-1.0)
+        out(0, 3 * R, ["yyl"])
+
+    def last_r():
+        newton(2, 2, T.r2[:, 0:R], "r2.own", T.r3[:], "r3")
+        dma("y", T.inv[:], T.r3[:], ["r3"], ["inv"])
+
+    extra = {("E", i): [later(out, s * R, (s + 1) * R, ["yy%d" % s])] for i, s in enumerate((4, 5, 6, 7, 8, 9, 3))}
+    extra["F", 8] = [last_r, later(opened, 3, 5)]
+    extra["E", 8] = [later(scale, 3, 8, T.rj2, "rj2", T.l3[:, R:2 * R], "l31"), later(opened, 3, 2)]
+    extra["E", 7] = [later(scale, 3, 7, T.rj2, "rj2", T.l3[:, 2 * R:3 * R], "l32"), later(opened, 3, 3)]
+    extra["E", 6].append(later(opened, 3, 4))
+    extra["E", CFG["low"]].append(lower)
+    items(3, rest + upper, ys, extra, CFG["lag3"])
 
     for q in ("v", "s", "t", "g", "sent"):
         wait("g", (q, cnt[q], {}))
-    for a in ARR:
+    for a in sent:
         wait("g", ("a_" + a, arrive, {}))
     for i in range(cnt["d"]):
         wait("g", ("d%d" % i, 16, {}))

@@ -6,17 +6,9 @@ HB = 8 * R
 HS = 8 * H
 WN = HB + NB * HS
 ZC = R + NB * H
-NP = 8
 CFG = {
-    "out": {1: "vvvvvv-", 2: "vvvvvv-", 3: "vvvvvvv"},
-    "eng": 4,
-    "cut": (0, 2, 4, 6),
-    "shipq": "sss",
-    "low": 6,
-    "newton": (("F", 1), ("S", 0)),
-    "lag1": dict(G=0, F=0, D=2, S=2, E=3),
-    "lag2": dict(G=0, F=0, D=2, S=2, E=3),
-    "lag3": dict(G=0, F=0, D=2, S=2, E=3),
+    "far": (5,), "halves": (5,), "gu": 28,
+    "eng": {"": (4, 4), "c0": (2, 2)},
 }
 
 
@@ -27,22 +19,21 @@ def _sb(dtype, **shapes):
 SCRATCH = {}
 SCRATCH.update(_sb("int32", colraw=[R], shp=[12], spt=[72], pi=[1], pt=[2], nvi=[72], ki=[72], sps=[72], blk=[72],
                    tsl=[72], cs=[72]))
-SCRATCH.update(_sb("uint16", shp16=[12], stg=[3, 7, 4], vl=[84], lb=[24], lc=[36], list2=[72], prm=[72], unperm=[72], rl=[72],
-                   ls=[576]))
-SCRATCH.update(_sb("float16", csg=[NB * H], colh=[12, 2, 16], q4=[4 * 128], sel=[2 * 128], c3=[72, 9], off=[72], idh=[128]))
-SCRATCH.update(_sb("bfloat16", vsend=[NB * 7 * H], eq=[576, 6], ones=[128], idb=[128], negb=[128], upb=[128], dnb=[128],
-                   idw=[6 * 128], al=[3 * R], nal=[3 * R], w1=[WN]))
-SCRATCH.update(_sb("float32", cw=[2 * ZC], csend=[2 * NB * H], pf=[8], sptf=[72], ext=[120],
-                   cl=[24, 16], cmpx=[96], nvf=[72], spf=[72], srt=[72], tmp=[72], tsf=[72], strd=[216], base=[72], ta=[72],
-                   istr=[72], bq=[72], fin=[576], rk2=[72], rk3=[72], gu=[72 * 16], tu=[72, 16],
+SCRATCH.update(_sb("uint16", shp16=[12], vl=[84], lb=[24], list2=[72], prm=[72], unperm=[72], rl=[72], ls=[576]))
+SCRATCH.update(_sb("float16", csg=[NB * H], colh=[12, 2, 16], q4=[4 * 128], sel=[2 * 128], c3=[72, 9], off=[72], idh=[128],
+                   negh=[128], ab=[2 * 432], gu=[72 * 16], tu=[72, 16]))
+SCRATCH.update(_sb("bfloat16", vsend=[NB * 7 * H], eq=[24, 24, 6], tb=[128], ti=[128], tm=[128], idb=[128], negb=[128],
+                   idw=[6 * 128], zero=[432], two=[128], al=[3 * R], nal=[4 * R], w1=[WN]))
+SCRATCH.update(_sb("float32", cw=[2 * ZC], csend=[2 * NB * H], pf=[8], shpf=[12], stg=[3, 7, 4], ext=[72], neg2=[128], sq=[R],
+                   cl=[24, 16], cmpx=[96], nvf=[72], spf=[72], srt=[72], tmp=[72], tsf=[72], base=[72], ta=[72],
+                   istr=[72], bq2=[3, 2, 24], sd2=[3, 2, 24], fin=[576], rk2=[72], rk3=[72],
                    negf=[128], idf=[128], w2=[WN], w3=[WN], r1=[ZC], r2=[ZC], r3=[R], rsend=[NB * H],
-                   rj1=[2 * R], rj2=[2 * R], nl0=[R], l3=[3 * R], gg=[15 * R], pp=[NP * R], snd2=[NB * 6 * H],
+                   rj1=[2 * R], rj2=[2 * R], nl0=[2 * R], l3=[3 * R], gg=[15 * R], p0=[9 * R], p2=[7 * R], snd2=[NB * 6 * H],
                    snd3=[NB * 6 * H], yy=[10 * R]))
 for _n in ("x1", "x2", "a0", "a1", "a2", "a4", "a5"):
     SCRATCH[_n] = ("psum", [128, 512], "float32")
 SCRATCH["a3"] = ("psum", [128, 16, 32], "float32")
-NPIECE = len(CFG["cut"]) - 1
-ARR = ["c0", "v0", "r2"] + ["x%d%d" % (k, i) for k in (2, 3) for i in range(6)]
+ARR = ["c0", "v0", "r2"] + ["x%d%d" % (k, i) for k in (2, 3) for i in range(3)]
 SEMAPHORES = ["v", "s", "t", "g", "sent"] + ["a_" + a for a in ARR] + ["d%d" % i for i in range(24)]
 
 
@@ -57,7 +48,6 @@ def rank_program(g, core, T, topo):
     cnt = {"v": 0, "s": 0, "t": 0, "g": 0, "sent": 0, "d": 0}
     clock = {q: {} for q in Q}
     writer, readers = {}, {}
-    npiece = len(CFG["cut"]) - 1
 
     def wait(q, tok):
         sem, n, clk = tok[0], tok[1], tok[2]
@@ -113,32 +103,30 @@ def rank_program(g, core, T, topo):
         Q[q].dma_start(out, in_).then_inc(T.sem[sem], 16)
         after((sem, 16, dict(clock[q]), "dma"), rd, wr)
 
-    def plan(src):
+    def plan(src, name):
         dsts = [c for c in T.cores if c != src]
         far = [c for c in dsts if topo.chip(c) != topo.chip(src)]
         near = [c for c in dsts if c not in far]
         used, out = [], {}
-        for grp in (far, near):
+        for grp, n in zip((far, near), CFG["eng"].get(name, CFG["eng"][""])):
             if not grp:
                 continue
             free = [e for e in topo.engines(src, grp[0]) if e not in used]
-            n = CFG["eng"]
             while n * len(grp) > len(free):
                 n //= 2
             step = len(free) // n
             for i, c in enumerate(grp):
-                out[c] = free[i::step][:n]
+                out[c] = free[i * (step // len(grp))::step][:n]
             used += free
         return out
 
-    mine = plan(core)
     others = [p for p in range(N) if p != rank]
-    arrive = sum(len(plan(T.cores[p])[core]) for p in others)
-    sent = []
+    arrive = {a: sum(len(plan(T.cores[p], a)[core]) for p in others) for a in ARR}
 
     def send(name, src, width, dst, rd):
         before("g", rd, [], True)
         tr = []
+        mine = plan(core, name)
         for b, p in enumerate(others):
             c = T.cores[p]
             rid, pid = topo.addr(c)[0:2]
@@ -148,10 +136,9 @@ def rank_program(g, core, T, topo):
                                         remote_sem=T.sem["a_" + name], src=src(b * width, (b + 1) * width), dst=dst(me)))
             cnt["sent"] += len(mine[c])
         g.remote_dma_fused(tr, local_sem=T.sem.sent)
-        sent.append(name)
 
     for a in ARR:
-        writer["arr." + a] = ("a_" + a, arrive, {}, "far")
+        writer["arr." + a] = ("a_" + a, arrive[a], {}, "far")
 
     V, S = g.vector, g.scalar
 
@@ -167,19 +154,19 @@ def rank_program(g, core, T, topo):
     def cp(out, a, rd, wr):
         op("v", lambda: V.tensor_copy(out, a), rd, wr)
 
-    def act(out, a, rd, wr, scale=1.0, bias=0.0):
+    def act(out, a, rd, wr, f=F.Identity, scale=1.0, bias=0.0):
         if scale == 1.0 and bias == 0.0:
-            op("s", lambda: S.activation(out, a, F.Copy), rd, wr)
+            op("s", lambda: S.activation(out, a, F.Copy if f == F.Identity else f), rd, wr)
         else:
-            op("s", lambda: S.activation(out, a, F.Identity, bias=bias, scale=scale), rd, wr)
+            op("s", lambda: S.activation(out, a, f, bias=bias, scale=scale), rd, wr)
 
     def third(buf, t):
         return buf[:, 24 * t:24 * t + 24]
 
     BANK = {n: T[n] for n in ("x1", "x2", "a0", "a1", "a2", "a3", "a4", "a5")}
 
-    def row(n):
-        return T.a3[:, 0:R // 32, :] if n == "a3" else BANK[n][:, 0:R]
+    def row(n, c0=0, c1=R):
+        return T.a3[:, c0 // 32:c1 // 32, :] if n == "a3" else BANK[n][:, c0:c1]
 
     dma("y", T.colraw[0:128:2, :], T.col[:, 2 * R:10 * R], [], ["colA"])
     dma("s", T.shp[:], T.ship[:], [], ["shp"])
@@ -188,22 +175,14 @@ def rank_program(g, core, T, topo):
     dma("y", T.w1[:, R:HB], T.val[:, 3 * R:10 * R], [], ["w1.own"])
     dma("y", T.al[:], T.val[:, 0:3 * R], [], ["al"])
 
-    op("v", lambda: V.memset(T.ones[:], 1.0), [], ["ones"])
+    def table(buf, key, pattern):
+        op("g", lambda: g.iota(buf[:], pattern, 0, -1, allow_small_or_imprecise_dtypes=True), [], [key])
+
+    table(T.tb, "tb", [[32, 4], [0, 2], [1, 16]])
     op("g", lambda: g.iota(T.pi[:], [[0, 1]], 0, 1), [], ["pi"])
-    op("g", lambda: g.affine_select(T.idb[:], T.ones[:], [[-1, 128]], A.is_equal, 0.0, 0, 1), ["ones"], ["idb"])
-    op("g", lambda: g.affine_select(T.upb[:], T.ones[:], [[-1, 128]], A.is_equal, 0.0, 16, 1), ["ones"], ["upb"])
-    op("g", lambda: g.affine_select(T.dnb[:], T.ones[:], [[-1, 128]], A.is_equal, 0.0, -16, 1), ["ones"], ["dnb"])
+    table(T.ti, "ti", [[1, 128]])
+    table(T.tm, "tm", [[32, 4], [128, 2], [1, 16]])
     op("g", lambda: g.iota(T.nvi[:], [[0, 3], [16, 24]], 0, 1), [], ["nvi"])
-    op("v", lambda: V.memset(T.w1[:, 0:R], 0.0), [], ["w1.z0"])
-    for b in range(NB):
-        op("v", lambda: V.memset(T.w1[:, HB + b * HS:HB + b * HS + H], 0.0), [], ["w1.z%d" % (b + 1)])
-    ts(T.pt[:, 0:1], T.pi[:], 4, None, A.logical_shift_right, None, ["pi"], ["pt0"])
-    ts(T.pt[:, 1:2], T.pi[:], 4, 1, A.logical_shift_right, A.bitwise_and, ["pi"], ["pt1"])
-    M0, M1, PH = [T.pf[:, i:i + 1] for i in range(3)]
-    ts(PH, T.pt[:, 0:1], 16.0, None, A.mult, None, ["pt0"], ["ph"])
-    ts(M0, T.pt[:, 1:2], -1.0, 1.0, A.mult, A.add, ["pt1"], ["m0"])
-    ts(M1, T.pt[:, 1:2], 1.0, None, A.mult, None, ["pt1"], ["m1"])
-    cp(T.idh[:], T.idb[:], ["idb"], ["idh"])
 
     def move(e, f):
         return T.q4[:, (2 * e + f) * 128:(2 * e + f + 1) * 128]
@@ -211,376 +190,446 @@ def rank_program(g, core, T, topo):
     def both(e):
         return T.sel[:, e * 128:(e + 1) * 128]
 
-    for e, f, src, key in ((0, 0, T.idb, "idb"), (1, 1, T.idb, "idb"), (0, 1, T.upb, "upb"), (1, 0, T.dnb, "dnb")):
-        ts(move(e, f), src[:], (M0, M1)[e], None, A.mult, None, [key, "m0", "m1"], ["q%d%d" % (e, f)])
+    def diag(q, out, key, x):
+        if q == "s":
+            act(out, T.idb[:], ["idb"], [key], scale=x)
+        else:
+            ts(out, T.ti[:], 0.0, x, A.is_equal, A.mult, ["ti"], [key])
+
+    def weights(q, ws):
+        for w in ws:
+            diag(q, T.idw[:, w * 128:(w + 1) * 128], "idw%d" % w, float(H * (w + 2)))
+
+    op("v", lambda: V.memset(T.zero[:], 0.0), [], ["zero"])
     for e in range(2):
-        tt(both(e), move(e, 0), move(e, 1), A.add, ["q%d0" % e, "q%d1" % e], ["sel%d" % e])
-    ts(T.nvf[:], T.nvi[:], PH, 1.0 / R, A.subtract, A.mult, ["nvi", "ph"], ["nvf"])
+        ts(both(e), T.tb[:], -16.0 * e, None, A.is_equal, None, ["tb"], ["sel%d" % e])
+    ts(T.pt[:, 0:1], T.pi[:], 4, None, A.logical_shift_right, None, ["pi"], ["pt0"])
+    ts(T.pt[:, 1:2], T.pi[:], 4, 1, A.logical_shift_right, A.bitwise_and, ["pi"], ["pt1"])
+    M1, PH = [T.pf[:, i:i + 1] for i in range(2)]
+    diag("v", T.idb[:], "idb", 1.0)
+    diag("v", T.idh[:], "idh", 1.0)
+    ts(PH, T.pt[:, 0:1], 16.0, None, A.mult, None, ["pt0"], ["ph"])
+    ts(M1, T.pt[:, 1:2], 1.0, None, A.mult, None, ["pt1"], ["m1"])
+    weights("s", (0, 1, 2))
+    for e in range(2):
+        for f in range(2):
+            ts(move(e, f), T.tm[:], 128.0 * f - 16.0 * e, None, A.is_equal, None, ["tm"], ["q%d%d" % (e, f)])
     mv = ["q00", "q01", "q10", "q11"]
-    act(T.idf[:], T.idb[:], ["idb"], ["idf"])
-    act(T.negf[:], T.idb[:], ["idb"], ["negf"], scale=-1.0)
-    act(T.negb[:], T.idb[:], ["idb"], ["negb"], scale=-1.0)
-    for w in range(6):
-        act(T.idw[:, w * 128:(w + 1) * 128], T.idb[:], ["idb"], ["idw%d" % w], scale=float(H * (w + 2)))
+    ts(T.nvf[:], T.nvi[:], PH, 1.0 / R, A.subtract, A.mult, ["nvi", "ph"], ["nvf"])
+    for buf, key, x in ((T.idf, "idf", 1.0), (T.negf, "negf", -1.0), (T.neg2, "neg2", -2.0)):
+        diag("s", buf[:], key, x)
 
     col = ["colA", "colB"]
+    cp(T.shpf[:], T.shp[:], ["shp"], ["shpf"])
     cp(T.shp16[:], T.shp[:], ["shp"], ["shp16"])
+    stg = ["stg%d" % w for w in range(7)]
+
+    def planes(ws):
+        for w in ws:
+            act(T.stg[:, :, w, :], T.shpf[:], ["shpf"], [stg[w]], bias=float(w * R))
+
+    planes(range(4))
     cp(T.csg[:], T.colraw[:, 0:R].indirect(T.shp16[:, 0:12]), col + ["shp16"], ["csg"])
     mm([(T.a0[:, e:2 * NB * H:2], both(e), T.csg[:]) for e in range(2)], ["csg", "sel0", "sel1"], ["Pa0"], True)
     act(T.csend[:], T.a0[:, 0:2 * NB * H], ["Pa0"], ["csend"])
     send("c0", lambda a, b: T.csend[:, a:b], 2 * H, lambda b: T.cw[:, 2 * (R + b * H):2 * (R + (b + 1) * H)], ["csend"])
     cp(T.colh[:], T.colraw[:], col, ["colh"])
-    cp(T.sptf[:], T.spt[:], ["spt"], ["sptf"])
     for e in range(2):
         mm([(T.a3[:, 0:12, 16 * e:16 * e + 16], move(e, f), T.colh[:, :, f, :]) for f in range(2)], mv + ["colh"], ["Pa3"])
     for e in range(2):
         mm([(row("a%d" % (1 + e)), both(e), T.colh[:])], ["colh", "sel%d" % e], ["Pa%d" % (1 + e)])
-    stg = ["stg%d" % w for w in range(7)]
-    for w in range(7):
-        ts(T.stg[:, :, w, :], T.shp[:], float(w * R), None, A.add, None, ["shp"], [stg[w]])
-    cp(T.vl[:], T.stg[:], stg, ["vl"])
     for t in range(3):
-        act(third(T.spf, t), third(T.sptf, t), ["sptf"], ["spf%d" % t], scale=1.0 / 1024, bias=3.0 + t / 4096.0)
+        ts(third(T.spf, t), third(T.spt, t), 1.0 / 1024, 3.0 + t / 4096.0, A.mult, A.add, ["spt"], ["spf%d" % t])
+    planes(range(4, 7))
+    weights("v", (3, 4, 5))
     op("v", lambda: V.transpose(T.cl[:], row("a3")), ["Pa3"], ["cl"])
-    act(T.vsend[:], T.w1[:, R:HB].indirect(T.vl[:, 0:84]), ["w1.own", "vl"], ["vsend"])
-    send("v0", lambda a, b: T.vsend[:, a:b], 7 * H, lambda b: T.w1[:, HB + b * HS + H:HB + (b + 1) * HS], ["vsend"])
-    for k, W in ((2, T.w2), (3, T.w3)):
-        op("g", lambda: g.iota(W[:, 0:2 * R], [[0, 2 * R]], 0, 0, allow_small_or_imprecise_dtypes=True), [], ["w%d.z0" % k])
-        for b in range(NB):
-            op("g", lambda: g.iota(W[:, HB + b * HS:HB + b * HS + 2 * H], [[0, 2 * H]], 0, 0,
-                                   allow_small_or_imprecise_dtypes=True), [], ["w%d.z%d" % (k, b + 1)])
-    for e in range(2):
-        act(T.cw[:, e:2 * R:2], row("a%d" % (1 + e)), ["Pa%d" % (1 + e)], ["cw%d" % e])
-
-    k0, k1, k2 = [third(T.ext, t + 1) for t in range(3)]
-    s0, s1, s2 = [third(T.srt, t) for t in range(3)]
-    m0, m1, m2 = [third(T.tmp, t) for t in range(3)]
-    for t in range(3):
-        tt(third(T.ext, t + 1), T.cl[:, :, 2 * t + 1], third(T.spf, t), A.add, ["cl", "spf%d" % t], ["k%d" % t])
-    key = ["k0", "k1", "k2"]
-    tt(m1, k0, k1, A.max, key[0:2], ["tm1"])
-    tt(m0, k0, k1, A.min, key[0:2], ["tm0"])
-    tt(m2, m1, k2, A.min, ["tm1", "k2"], ["tm2"])
-    tt(s0, m0, k2, A.min, ["tm0", "k2"], ["s0"])
-    tt(s2, m1, k2, A.max, ["tm1", "k2"], ["s2"])
-    tt(s1, m0, m2, A.max, ["tm0", "tm2"], ["s1"])
-    cp(T.c3[:, 0:24, 0:7], T.cl[:, :, 2:16:2], ["cl"], ["c30"])
-    ts(T.ki[:], T.srt[:], 4096.0, None, A.mult, None, ["s0", "s1", "s2"], ["ki"])
-    cp(T.c3[:, 24:48, 0:7], T.cl[:, :, 2:16:2], ["cl"], ["c31"])
-    ts(T.sps[:], T.ki[:], 2, 1023, A.logical_shift_right, A.bitwise_and, ["ki"], ["sps"])
-    ts(T.tsl[:], T.ki[:], 3, None, A.bitwise_and, None, ["ki"], ["tsl"])
-    ts(T.off[:], T.sps[:], 2.0, M1, A.mult, A.add, ["sps", "m1"], ["off"])
-    cp(T.c3[:, 48:72, 0:7], T.cl[:, :, 2:16:2], ["cl"], ["c32"])
-    for e in range(2):
-        mm([(T.a4[:, e:72:2], move(e, f), T.off[:, f:72:2]) for f in range(2)], mv + ["off"], ["Pa4"])
-    tt(T.tsf[:], T.tsl[:], T.nvf[:], A.add, ["tsl", "nvf"], ["tsf"])
-    ts(T.blk[:], T.ki[:], 8, 15, A.logical_shift_right, A.bitwise_and, ["ki"], ["blk"])
-    ts(T.prm[:], T.tsf[:], float(R), 0.25, A.mult, A.add, ["tsf"], ["prm"])
-    cp(T.list2[:], T.a4[:, 0:72], ["Pa4"], ["list2"])
-    act(T.nal[:], T.al[:, 0:3 * R].indirect(T.prm[:, 0:72]), ["al", "prm"], ["nal"], scale=-1.0)
+    act(T.cw[:, 1:2 * R:2], row("a2"), ["Pa2"], ["cw1"])
 
     JOINS = [3] * 7 + [2, 1]
-    LIST = [72 * i for i in range(8)] + [552]
-    CB = [("x1", 0), ("x2", 0), ("a0", 0), ("a1", 0), ("a2", 0), ("a4", 0), ("a5", 0), ("a0", 0), ("a0", 288)]
+    FAR = CFG["far"]
+    CB = [("x1", 0), ("x2", 0), ("a0", 0), ("a1", 0), ("a2", 0), ("a4", 0), None, None, None]
 
     def spread(i):
         s = (i + 1 if i < 6 else 0) if i < 7 else 15 - i
-        n = 24 * JOINS[i]
         bk, o = CB[i]
-        mm([(BANK[bk][:, o + w:o + 6 * n:6], T.idh[:], T.c3[:, 0:n, s]) for w in range(6)],
-           (["c30", "c31", "c32"] if i < 7 else ["c3a", "c3b", "c3c"]) + ["idh"], ["P" + bk], True)
+        calls = [(BANK[bk][:, o + w:o + 144 * JOINS[i]:6], T.idh[:], T.c3[:, 0:24 * JOINS[i], s]) for w in range(6)]
+        rd = ["idh"] + (["c30", "c31", "c32"] if i < 7 else ["c3a", "c3b", "c3c"])
+        if i in FAR:
+            mm([(BANK[bk][:, 0:432], T.idb[:], T.zero[:])] + calls, rd + ["idb", "zero"], ["P" + bk], stop=False)
+        else:
+            mm(calls, rd, ["P" + bk], True)
 
-    for i in range(6):
-        spread(i)
-    ts(T.ta[:], T.blk[:], 6.0, float(HS - H), A.is_ge, A.mult, ["blk"], ["ta"])
-    ts(T.cs[:], T.ki[:], 12, None, A.logical_shift_right, None, ["ki"], ["cs"])
-    tt(T.ta[:], T.ta[:], T.blk[:], A.mult, ["ta", "blk"], ["ta"])
-    ts(T.istr[:], T.blk[:], 6.0, H / R, A.is_ge, A.max, ["blk"], ["istr"])
-    ts(T.strd[:, 0:72], T.blk[:], 6.0, H / R, A.is_lt, A.max, ["blk"], ["strd"])
-    tt(T.base[:], T.ta[:], T.sps[:], A.add, ["ta", "sps"], ["base"])
+    k0, k1, k2 = [third(T.ext, t) for t in range(3)]
+    s0, s1, s2 = [third(T.srt, t) for t in range(3)]
+    m0, m1, m2 = [third(T.tmp, t) for t in range(3)]
+    diag("v", T.negb[:], "negb", -1.0)
+    diag("v", T.negh[:], "negh", -1.0)
+    diag("v", T.two[:], "two", 2.0)
+    for t in range(3):
+        tt(third(T.ext, t), T.cl[:, :, 2 * t + 1], third(T.spf, t), A.add, ["cl", "spf%d" % t], ["k%d" % t])
+    key = ["k0", "k1", "k2"]
+    cp(T.c3[:, 0:24, 0:7], T.cl[:, :, 2:16:2], ["cl"], ["c30"])
+    tt(m1, k0, k1, A.max, key[0:2], ["tm1"])
+    tt(m0, k0, k1, A.min, key[0:2], ["tm0"])
+    cp(T.vl[:], T.stg[:], stg, ["vl"])
+    cp(T.c3[:, 24:48, 0:7], T.cl[:, :, 2:16:2], ["cl"], ["c31"])
+    act(T.vsend[:], T.w1[:, R:HB].indirect(T.vl[:, 0:84]), ["w1.own", "vl"], ["vsend"])
+    send("v0", lambda a, b: T.vsend[:, a:b], 7 * H, lambda b: T.w1[:, HB + b * HS + H:HB + (b + 1) * HS], ["vsend"])
+    for k, W, n in ((1, T.w1, 1), (2, T.w2, 2), (3, T.w3, 2)):
+        op("g", lambda: g.iota(W[:, 0:n * R], [[0, n * R]], 0, 0, allow_small_or_imprecise_dtypes=True), [], ["w%d.z0" % k])
+        for b in range(NB):
+            op("g", lambda: g.iota(W[:, HB + b * HS:HB + b * HS + n * H], [[0, n * H]], 0, 0,
+                                   allow_small_or_imprecise_dtypes=True), [], ["w%d.z%d" % (k, b + 1)])
+    tt(m2, m1, k2, A.min, ["tm1", "k2"], ["tm2"])
+    tt(s2, m1, k2, A.max, ["tm1", "k2"], ["s2"])
+    tt(s0, m0, k2, A.min, ["tm0", "k2"], ["s0"])
+    tt(s1, m0, m2, A.max, ["tm0", "tm2"], ["s1"])
+    cp(T.cw[:, 0:2 * R:2], row("a1"), ["Pa1"], ["cw0"])
+    ts(T.ki[:], T.srt[:], 4096.0, None, A.mult, None, ["s0", "s1", "s2"], ["ki"])
     cp(T.lb[:], T.stg[:, :, 0:2, :], stg, ["lb"])
-    tt(T.bq[:], T.base[:], T.istr[:], A.mult, ["base", "istr"], ["bq"])
-    cp(T.lc[:], T.stg[:, :, 0:3, :], stg, ["lc"])
-    cp(T.rl[:], T.sps[:], ["sps"], ["rl"])
-    for o, n in ((72, 72), (144, 48), (192, 24)):
-        cp(T.strd[:, o:o + n], T.strd[:, 0:n], ["strd"], ["strd%d" % o])
-    strd = ["strd", "strd72", "strd144", "strd192"]
-    ts(T.c3[:, 0:24, 7], third(T.cs, 1), -3.0, None, A.add, None, ["cs"], ["c3a"])
-    ts(T.c3[:, 0:24, 8], third(T.cs, 2), -3.0, None, A.add, None, ["cs"], ["c3b"])
-    ts(T.c3[:, 24:48, 8], third(T.cs, 2), -3.0, None, A.add, None, ["cs"], ["c3c"])
-    cp(T.ext[:, 0:24], k2, ["k2"], ["ext0"])
-    cp(T.ext[:, 96:120], k0, ["k0"], ["ext1"])
-    tt(T.cmpx[:], T.ext[:, 0:96], T.ext[:, 24:120], A.is_gt, key + ["ext0", "ext1"], ["cmpx"])
-    tt(T.rk2[:], T.cmpx[:, 24:96], T.cmpx[:, 0:72], A.subtract, ["cmpx"], ["rk2"])
-    tt(T.rk3[:], T.rk2[:], T.nvf[:], A.add, ["rk2", "nvf"], ["rk3"])
-    ts(T.unperm[:], T.rk3[:], float(R), R + 0.25, A.mult, A.add, ["rk3"], ["unperm"])
+    cp(T.c3[:, 48:72, 0:7], T.cl[:, :, 2:16:2], ["cl"], ["c32"])
+    for i in (0, 1, 2):
+        spread(i)
+    ts(T.sps[:], T.ki[:], 2, 1023, A.logical_shift_right, A.bitwise_and, ["ki"], ["sps"])
+    ts(T.tsl[:], T.ki[:], 3, None, A.bitwise_and, None, ["ki"], ["tsl"])
+    ts(T.blk[:], T.ki[:], 8, 15, A.logical_shift_right, A.bitwise_and, ["ki"], ["blk"])
+    ts(T.off[:], T.sps[:], 2.0, M1, A.mult, A.add, ["sps", "m1"], ["off"])
+    for e in range(2):
+        mm([(T.a4[:, e:72:2], move(e, f), T.off[:, f:72:2]) for f in range(2)], mv + ["off"], ["Pa4"])
+    tt(T.tsf[:], T.tsl[:], T.nvf[:], A.add, ["tsl", "nvf"], ["tsf"])
+    ts(T.ta[:], T.blk[:], 6.0, float(HS - H), A.is_ge, A.mult, ["blk"], ["ta"])
+    ts(T.istr[:], T.blk[:], 6.0, H / R, A.is_ge, A.max, ["blk"], ["istr"])
+    ts(T.prm[:], T.tsf[:], float(R), 0.25, A.mult, A.add, ["tsf"], ["prm"])
+    tt(T.ta[:], T.ta[:], T.blk[:], A.mult, ["ta", "blk"], ["ta"])
+    cp(T.list2[:], T.a4[:, 0:72], ["Pa4"], ["list2"])
+    act(T.nal[:, R:4 * R], T.al[:, 0:3 * R].indirect(T.prm[:, 0:72]), ["al", "prm"], ["nal"], scale=-1.0)
+    for i in (3, 4, 5):
+        spread(i)
+    ts(T.sd2[:, :, 0, :], T.blk[:], 6.0, H / R, A.is_lt, A.max, ["blk"], ["sd0"])
+    tt(T.base[:], T.ta[:], T.sps[:], A.add, ["ta", "sps"], ["base"])
+    ts(T.sd2[:, :, 1, :], T.blk[:], 6.0, H / R, A.is_lt, A.max, ["blk"], ["sd1"])
+    ts(T.cs[:], T.ki[:], 12, None, A.logical_shift_right, None, ["ki"], ["cs"])
+    tt(T.bq2[:, :, 0, :], T.base[:], T.istr[:], A.mult, ["base", "istr"], ["bq0"])
 
     cwk = ["cw0", "cw1", "arr.c0", "list2"]
+    cut = (0, CFG["gu"], (72 + CFG["gu"]) // 4 * 2, 72)
     for j in range(3):
-        (act if j else cp)(T.gu[:, R * j:R * j + R], T.cw[:, 0:2 * ZC].indirect(third(T.list2, j)), cwk, ["gu%d" % j])
+        (act if j else cp)(T.gu[:, 16 * cut[j]:16 * cut[j + 1]], T.cw[:, 0:2 * ZC].indirect(T.list2[:, cut[j]:cut[j + 1]]), cwk, ["gu%d" % j])
+    cp(T.nal[:, 0:R], T.nal[:, R:2 * R], ["nal"], ["nal2"])
     for j in range(3):
-        op("v", lambda: V.transpose(T.tu[:, 24 * j:24 * j + 24, :], T.gu[:, R * j:R * j + R]), ["gu%d" % j], ["tu%d" % j])
+        op("v", lambda: V.transpose(T.tu[:, cut[j]:cut[j + 1], :], T.gu[:, 16 * cut[j]:16 * cut[j + 1]]), ["gu%d" % j], ["tu%d" % j])
+    cp(T.rl[:], T.sps[:], ["sps"], ["rl"])
+    tt(T.bq2[:, :, 1, :], T.base[:], T.istr[:], A.mult, ["base", "istr"], ["bq1"])
+
+    def block(i, j):
+        return 6 * (i // 2) + 2 * j + i % 2 if i < 6 else (18, 21, 23)[i - 6] + j
 
     def compare(i):
-        n = 24 * JOINS[i]
+        n, step = JOINS[i], 2 if i < 6 else 1
         bk, o = CB[i]
-        tt(T.eq[:, LIST[i]:LIST[i] + n, :], BANK[bk][:, o:o + 6 * n], T.tu[:, 0:n, 4:16:2], A.is_equal,
+        tt(T.eq[:, block(i, 0):block(i, n - 1) + 1:step, :, :], BANK[bk][:, o:o + 144 * n], T.tu[:, 0:24 * n, 4:16:2], A.is_equal,
            ["P" + bk, "tu0", "tu1", "tu2"], ["eq%d" % i])
 
-    GROUP = [(0, 1), (2, 3), (4, 5), (6, 7, 8)]
-    WB = ["a5", "a0", "a2", "a1"]
+    def differ(i):
+        bk, c = CB[i][0], 432 * (i % 2)
+        mm([(BANK[bk][:, 0:432], T.negh[:], T.tu[:, :, 4:16:2])], ["negh", "tu0", "tu1", "tu2", "P" + bk], ["P" + bk], start=False)
+        act(T.ab[:, c:c + 432], BANK[bk][:, 0:432], ["P" + bk], ["ab%d" % i], F.Abs)
+        act(T.eq[:, block(i, 0):block(i, 2) + 1:2, :, :], T.ab[:, c:c + 432], ["ab%d" % i], ["eq%d" % i], F.Relu, scale=-1.0, bias=1.0)
+
+    GROUP = [(0, 1), (2, 3), (4, 5), (6,), (7, 8)]
+    WB = ["a5", "a0", "a2", None, None]
+
+    def span(lg):
+        return block(GROUP[lg][0], 0), sum(JOINS[i] for i in GROUP[lg])
 
     def weigh(lg):
         B = BANK[WB[lg]]
-        calls = [(B[:, 0:144], T.idw[:, w * 128:(w + 1) * 128], T.eq[:, 144 * lg:144 * lg + 144, w]) for w in range(6)]
-        calls += [(B[:, LIST[i] - 144 * lg:LIST[i] - 144 * lg + 24 * JOINS[i]], T.idf[:], T.bq[:, 0:24 * JOINS[i]]) for i in GROUP[lg]]
-        mm(calls, ["eq%d" % i for i in GROUP[lg]] + ["idw%d" % w for w in range(6)] + ["idf", "bq"], ["P" + WB[lg]])
+        o, n = span(lg)
+        calls = [(B[:, 0:24 * n], T.idw[:, w * 128:(w + 1) * 128], T.eq[:, o:o + n, :, w]) for w in range(6)]
+        if lg < 3:
+            calls += [(B[:, 0:144], T.idf[:], T.bq2[:])]
+        else:
+            calls += [(B[:, 24 * (block(i, 0) - o):24 * (block(i, 0) - o + JOINS[i])], T.idf[:], T.bq2[:, 0:JOINS[i], 0, :])
+                      for i in GROUP[lg]]
+        mm(calls, ["eq%d" % i for i in GROUP[lg]] + ["idw%d" % w for w in range(6)] + ["idf", "bq0", "bq1"], ["P" + WB[lg]])
 
     def final(lg, step):
-        c = slice(144 * lg, 144 * lg + 144)
+        o, n = span(lg)
+        c = slice(24 * o, 24 * (o + n))
         if step == 0:
-            o = 72 if lg == 3 else 0
-            tt(T.fin[:, c], BANK[WB[lg]][:, 0:144], T.strd[:, o:o + 144], A.mult, ["P" + WB[lg]] + strd, ["fin%d" % lg])
+            parts = [(0, n, T.sd2[:])] if lg < 3 else [(block(i, 0) - o, JOINS[i], T.sd2[:, 0:JOINS[i], 0, :]) for i in GROUP[lg]]
+            for x, m, sd in parts:
+                tt(T.fin[:, 24 * (o + x):24 * (o + x + m)], BANK[WB[lg]][:, 24 * x:24 * (x + m)], sd, A.mult,
+                   ["P" + WB[lg], "sd0", "sd1"], ["fin%d.%d" % (lg, x)])
         else:
-            ts(T.ls[:, c], T.fin[:, c], float(R // H), 0.25, A.mult, A.add, ["fin%d" % lg], ["ls%d" % lg])
+            ts(T.ls[:, c], T.fin[:, c], float(R // H), 0.25, A.mult, A.add, ["fin%d.%d" % (lg, x) for x in (0, 2)], ["ls%d" % lg])
 
     WIN = {1: T.w1, 2: T.w2, 3: T.w3}
     WK = {1: ["w1.own", "arr.v0"] + ["w1.z%d" % i for i in range(4)]}
     for k in (2, 3):
         WK[k] = (["w%d.u%d" % (k, w) for w in range(6)] + ["w%d.z%d" % (k, i) for i in range(4)]
-                 + ["arr.x%d%d" % (k, i) for i in range(npiece)])
-    NL0 = {1: (T.nal[:, 0:R], "nal"), 2: (T.nal[:, 0:R], "nal"), 3: (T.nl0[:], "nl0")}
-    BANKS = {1: "a3 a5 a0 a1 a4 a2 a5 a3 x1".split(), 2: "a4 a2 a0 a1 a3 a4 a1 a0 a2".split(),
-             3: "a2 a0 a5 a4 a3 a1 a3 a4 a5".split()}
-    st = {"p": 0}
-    prods = {}
+                 + ["arr.x%d%d" % (k, i) for i in range(3)])
+    NL0 = {1: (T.nal, ["nal2", "nal"]), 2: (T.nal, ["nal2", "nal"]), 3: (T.nl0, ["nl0", "nl02"])}
+    BANKS = {1: {8: "x1"}, 2: {}, 3: {}}
+    queue = ([(1, i) for i in range(6)] + [("c", 6), ("c", 7), ("w", 3), ("w", 4), (1, 7), (1, 6), (1, 9)]
+             + [(2, i) for i in (0, 1, 2, 3, 4, 5, 8, 7, 6, 9)] + [(3, i) for i in (8, 7, 6, 0, 1, 2, 3, 4, 5)])
+    free = []
+    X2 = {1: "x2"}
 
-    def window(k, i, j0, j1):
-        return (WIN[k][:, 0:WN].indirect(T.ls[:, LIST[i] + 24 * j0:LIST[i] + 24 * j1]), WK[k] + ["ls%d" % min(i // 2, 3)])
+    def release(b):
+        free.append(b)
+        while free and queue:
+            k, i = queue[0]
+            fit = [x for x in free if x != "a3" or k not in ("c", "w")]
+            if not fit:
+                return
+            queue.pop(0)
+            free.remove(fit[0])
+            if k == "c":
+                for j in ((6,), (7, 8))[i - 6]:
+                    CB[j] = (fit[0], 288 if j == 8 else 0)
+                    spread(j)
+            elif k == "w":
+                WB[i] = fit[0]
+            else:
+                BANKS[k][i] = fit[0]
+                if i != 8:
+                    opened(k, i)
 
-    def newprod(i, j):
-        p = st["p"] % NP
-        st["p"] += 1
-        prods[i, j] = (T.pp[:, p * R:(p + 1) * R], "p%d" % p)
-        return prods[i, j]
+    def window(k, i, j, n):
+        o = 24 * block(i, j)
+        return WIN[k][:, 0:WN].indirect(T.ls[:, o:o + 24 * n]), WK[k] + ["ls%d" % (i // 2 if i < 7 else 4)]
 
     def got(i, j):
-        return T.gg[:, (2 * i + j - 1) * R:(2 * i + j) * R], "g%d" % i
+        c = 4 * (i // 2) + 2 * (j - 1) + i % 2 if i < 6 else (12, 14)[i - 6] + j - 1
+        return c * R, "g%d" % c
 
-    def gather(k, i):
-        src, rd = window(k, i, 1, JOINS[i])
-        act(T.gg[:, 2 * i * R:(2 * i + JOINS[i] - 1) * R], src, rd, ["g%d" % i])
+    def gather(k, i, j, n):
+        src, rd = window(k, i, j, n)
+        c = got(i, j)[0]
+        act(T.gg[:, c:c + n * R], src, rd, ["g%d" % (c // R + x) for x in range(n)])
 
-    def fused(k, i):
-        src, rd = window(k, i, 0, 1)
-        p, pk = newprod(i, 0)
-        tt(p, src, NL0[k][0], A.mult, rd + [NL0[k][1]], [pk])
+    def fused(k, i, n=1):
+        src, rd = window(k, i, 0, n)
+        tt(T.p0[:, i * R:(i + n) * R], src, NL0[k][0][:, 0:n * R], A.mult, rd + NL0[k][1][0:n], ["p0%d" % x for x in range(i, i + n)])
+
+    def prod(i, j):
+        return (T.p0 if j == 0 else T.p2)[:, i * R:(i + 1) * R], "p%d%d" % (j, i)
 
     def opened(k, i):
         b = BANKS[k][i]
-        mm([(row(b), T.idb[:], T.w1[:, 0:R])], ["idb", "w1.z0"], ["P" + b], stop=False)
+        mm([(row(b), T.idb[:], T.zero[:, 0:R])], ["idb", "zero"], ["P" + b], stop=False)
 
     def direct(k, i):
         b = BANKS[k][i]
-        u, uk = got(i, 1)
-        tt(row(b), u, row("x1"), A.mult, [uk, "Px1"], ["P" + b])
+        c, uk = got(i, 1)
+        tt(row(b), T.gg[:, c:c + R], row("x1"), A.mult, [uk, "Px1"], ["P" + b])
 
     def second(k, i):
-        u, uk = got(i, 2)
-        p, pk = newprod(i, 2)
-        tt(p, u, row("x2"), A.mult, [uk, "Px2"], [pk])
+        c, uk = got(i, 2)
+        tt(prod(i, 2)[0], T.gg[:, c:c + R], row(X2[k]), A.mult, [uk, "P" + X2[k]], [prod(i, 2)[1]])
 
-    def total(k, i, js):
+    def total(k, i):
         b = BANKS[k][i]
         if i < 7:
             c = (2 + i) * R if i < 6 else R
             calls = [(row(b), T.idb[:], T.w1[:, c:c + R])]
         else:
-            calls = [(row(b), T.idb[:] if b == "x1" else T.negb[:], T.nal[:, (9 - i) * R:(10 - i) * R])]
-        calls += [(row(b), T.negf[:] if b == "x1" else T.idf[:], prods[i, j][0]) for j in js]
-        mm(calls, ["idb", "negb", "idf", "negf", "nal", "w1.own"] + [prods[i, j][1] for j in js] + ([] if i == 8 else ["P" + b]),
+            calls = [(row(b), T.idb[:] if b == "x1" else T.negb[:], T.nal[:, (10 - i) * R:(11 - i) * R])]
+        calls += [(row(b), T.negf[:] if b == "x1" else T.idf[:], prod(i, 0)[0])]
+        mm(calls, ["idb", "negb", "idf", "negf", "nal", "w1.own", prod(i, 0)[1]] + ([] if i == 8 else ["P" + b]),
            ["P" + b], start=(i == 8))
 
-    def evict(k, i, out, key):
+    def evict(k, i, out, key, c0=0, c1=R):
         b = BANKS[k][i]
-        if CFG["out"][k][i] == "s":
-            act(out, row(b), ["P" + b], [key])
-        else:
-            tt(out, row(b), prods[i, 2][0], A.add, ["P" + b, prods[i, 2][1]], [key])
+        tt(out if key else row(b), row(b, c0, c1), T.p2[:, i * R + c0:i * R + c1], A.subtract if k == 2 else A.add,
+           ["P" + b, prod(i, 2)[1]], [key or "P" + b])
+        if key and c1 == R:
+            release(b)
 
     def scale(k, i, rj, rk, out, ok):
         b = BANKS[k][i]
         tt(out, row(b), rj[:, (8 - i) * R:(9 - i) * R], A.mult, ["P" + b, rk], [ok])
+        release(b)
+
+    def ship(k, c):
+        SB = T.snd2 if k == 2 else T.snd3
+        w0, o = 2 * c, NB * 2 * c * H
+        key = "snd%d%d" % (k, c)
+        act(SB[:, o:o + NB * 2 * H], WIN[k][:, (2 + w0) * R:(4 + w0) * R].indirect(T.lb[:, 0:24]),
+            ["w%d.u%d" % (k, w0), "w%d.u%d" % (k, w0 + 1), "lb"], [key])
+        send("x%d%d" % (k, c), lambda a, b: SB[:, o + a:o + b], 2 * H,
+             lambda b: WIN[k][:, HB + b * HS + (2 + w0) * H:HB + b * HS + (4 + w0) * H], [key])
+
+    def newton(k):
+        b, n = BANKS[k][6], BANKS[k][9]
+        tt(row(n), row(b), T.sq[:], A.mult, ["P" + b, "sq"], ["P" + n])
+        release(b)
+        if k == 1:
+            mm([(row(n), T.two[:], T.w1[:, R:2 * R])], ["two", "w1.own", "P" + n], ["P" + n], start=False)
+        else:
+            mm([(row(n), T.neg2[:], T.r2[:, 0:R])], ["neg2", "r2.own", "P" + n], ["P" + n], start=False)
+
+    def new_r(k, out, ok):
+        n = BANKS[k][9]
+        act(out, row(n), ["P" + n], [ok], scale=-1.0, bias=4.0 if k == 1 else 0.0)
 
     def later(f, *a):
         return lambda: f(*a)
 
-    def ship(k, c, q):
-        SB = T.snd2 if k == 2 else T.snd3
-        w0, w1 = CFG["cut"][c], CFG["cut"][c + 1]
-        n, o = w1 - w0, NB * w0 * H
-        src = WIN[k][:, (2 + w0) * R:(2 + w1) * R].indirect((T.shp16, T.lb, T.lc)[n - 1][:, 0:12 * n])
-        key = "snd%d%d" % (k, c)
-        (act if q == "s" else cp)(SB[:, o:o + NB * n * H], src, ["w%d.u%d" % (k, w) for w in range(w0, w1)] + ["shp16", "lb", "lc"], [key])
-        send("x%d%d" % (k, c), lambda a, b: SB[:, o + a:o + b], n * H,
-             lambda b: WIN[k][:, HB + b * HS + (2 + w0) * H:HB + b * HS + (2 + w1) * H], [key])
+    def uppers(k, leave, extra, begun=False):
+        def also(x, p):
+            for f in extra.get((x, p), ()):
+                f()
 
-    def ships(k):
-        return {("E", CFG["cut"][c + 1] - 1): [later(ship, k, c, CFG["shipq"][c])] for c in range(npiece)}
+        def directs(p):
+            for i in (2 * p, 2 * p + 1):
+                direct(k, i); total(k, i)
+                also("D", i)
 
-    def newton(k, step, r, rk, out=None, ok=None):
-        b = BANKS[k][6]
-        P, pk = row(b), "P" + b
-        if step == 0:
-            tt(P, P, r, A.mult, [pk, rk], [pk])
-        elif step == 1:
-            act(P, P, [pk], [pk], scale=-1.0, bias=2.0)
-        else:
-            tt(out, P, r, A.mult, [pk, rk], [ok])
-
-    def items(k, order, dst, extra, lag):
-        def late(i):
-            return JOINS[i] < 3 or CFG["out"][k][i] == "v"
-
-        def stage(x, i):
-            if x == "F":
-                fused(k, i)
-                if JOINS[i] == 1:
-                    total(k, i, [0])
-            elif x == "E":
-                if dst(i):
-                    evict(k, i, *dst(i))
-            elif x == "S":
-                if JOINS[i] == 3:
-                    second(k, i)
-                    if not late(i):
-                        total(k, i, [0, 2])
-            elif JOINS[i] > 1:
-                if x == "G":
-                    gather(k, i)
-                else:
-                    direct(k, i)
-                    if late(i):
-                        total(k, i, [0])
-
-        for m in range(len(order) + max(lag.values())):
-            for x in lag:
-                if 0 <= m - lag[x] < len(order):
-                    i = order[m - lag[x]]
-                    stage(x, i)
-                    for f in extra.get((x, i), ()):
-                        f()
+        if not begun:
+            gather(k, 0, 1, 2)
+            if k == 1:
+                gather(k, 0, 2, 2)
+            fused(k, 0, 2)
+        also("F", 0)
+        directs(0)
+        gather(k, 2, 1, 2)
+        if k > 1:
+            gather(k, 0, 2, 2)
+        also("G", 0)
+        fused(k, 2, 2)
+        also("F", 1)
+        for p in range(3):
+            if p < 2:
+                directs(p + 1)
+            if p == 0:
+                gather(k, 4, 1, 2); gather(k, 2, 2, 2)
+            for i in (2 * p, 2 * p + 1):
+                second(k, i)
+                also("S", i)
+            for i in (2 * p, 2 * p + 1):
+                leave(i)
+            if p == 0:
+                gather(k, 4, 2, 2)
+                fused(k, 4, 2)
+            also("E", p)
 
     def up(k):
-        return lambda w: (WIN[k][:, (2 + w) * R:(3 + w) * R], "w%d.u%d" % (k, w))
-
-    def merged(*ds):
-        out = {}
-        for d in ds:
-            for x in d:
-                out.setdefault(x, []).extend(d[x])
-        return out
-
-    def opens(k, *pairs):
-        return {("E", e): [later(opened, k, i)] for e, i in pairs}
-
-    def rtable():
-        act(T.r1[:, 0:R], T.w1[:, R:2 * R], ["w1.own"], ["r1.own"], scale=-1.0, bias=2.0)
-        for b in range(NB):
-            c = HB + b * HS + H
-            act(T.r1[:, R + b * H:R + (b + 1) * H], T.w1[:, c:c + H], ["arr.v0"], ["r1.%d" % b], scale=-1.0, bias=2.0)
+        def leave(w):
+            evict(k, w, WIN[k + 1][:, (2 + w) * R:(3 + w) * R], "w%d.u%d" % (k + 1, w))
+            if w % 2:
+                ship(k + 1, w // 2)
+        return leave
 
     R1 = ["r1.own", "r1.0", "r1.1", "r1.2", "rl"]
     R2 = ["r2.own", "arr.r2", "rl"]
+
+    def own_r():
+        act(T.r1[:, 0:R], T.w1[:, R:2 * R], ["w1.own"], ["r1.own"], scale=-1.0, bias=2.0)
+
+    def far_r():
+        for b in range(NB):
+            c = HB + b * HS + H
+            ts(T.r1[:, R + b * H:R + (b + 1) * H], T.w1[:, c:c + H], -1.0, 2.0, A.mult, A.add, ["arr.v0"], ["r1.%d" % b])
+
+    def send_r():
+        act(T.rsend[:], T.r2[:, 0:R].indirect(T.shp16[:, 0:12]), ["r2.own", "shp16"], ["rsend"])
+        send("r2", lambda a, b: T.rsend[:, a:b], H, lambda b: T.r2[:, R + b * H:R + (b + 1) * H], ["rsend"])
 
     def minus_r(out, key, tab, rd):
         act(out[:], tab[:, 0:ZC].indirect(T.rl[:, 24:72]), rd, [key], scale=-1.0)
 
     def lowest(out, key, tab, rd):
-        tt(out, tab[:, 0:ZC].indirect(T.rl[:, 0:24]), T.nal[:, 0:R], A.mult, rd + ["nal"], [key])
+        tt(out, tab[:, 0:ZC].indirect(T.rl[:, 0:24]), T.nal[:, 0:R], A.mult, rd + ["nal2"], [key])
 
-    def rsend():
-        act(T.rsend[:], T.r2[:, 0:R].indirect(T.shp16[:, 0:12]), ["r2.own", "shp16"], ["rsend"])
-        send("r2", lambda a, b: T.rsend[:, a:b], H, lambda b: T.r2[:, R + b * H:R + (b + 1) * H], ["rsend"])
-
-    upper, rest = [0, 1, 2, 3, 4, 5], [8, 7, 6]
+    for i in FAR:
+        differ(i)
     compare(0); compare(1); weigh(0)
     for j in (1, 2):
-        mm([(row("x%d" % j), T.idb[:], T.nal[:, j * R:(j + 1) * R])], ["idb", "nal"], ["Px%d" % j])
-    rtable()
-    compare(2); final(0, 0); compare(3); weigh(1); final(0, 1)
-    opened(1, 0); opened(1, 1)
-    items(1, upper, up(2), merged(ships(2), {
-        ("F", 0): [later(compare, 4), later(final, 1, 0), later(opened, 1, 2), later(opened, 1, 3)],
-        ("F", 1): [later(compare, 5), later(weigh, 2), later(final, 1, 1), later(opened, 1, 4)],
-        ("D", 0): [later(final, 2, 0), later(opened, 1, 5)],
-        ("S", 0): [later(final, 2, 1)],
-        ("E", 1): [later(spread, 6)],
-        ("E", 2): [later(spread, 7), later(spread, 8)],
-    }, opens(1, (0, 7)), opens(2, (4, 0), (5, 1))), CFG["lag1"])
+        mm([(row("x%d" % j), T.idb[:], T.nal[:, (j + 1) * R:(j + 2) * R])], ["idb", "nal"], ["Px%d" % j])
+    compare(2); compare(3); weigh(1)
+    if 4 not in FAR:
+        compare(4)
+    final(0, 0)
+    ts(T.c3[:, 0:24, 7], third(T.cs, 1), -3.0, None, A.add, None, ["cs"], ["c3a"])
+    ts(T.c3[:, 0:24, 8], third(T.cs, 2), -3.0, None, A.add, None, ["cs"], ["c3b"])
+    ts(T.c3[:, 24:48, 8], third(T.cs, 2), -3.0, None, A.add, None, ["cs"], ["c3c"])
+    final(0, 1)
+    far_r()
+    release("a3"); release("a5")
+    uppers(1, up(1), {
+        ("F", 0): [later(final, 1, 0), later(release, "a0"), later(release, "a1"), later(weigh, 2), later(release, "a4")],
+        ("D", 0): [later(final, 1, 1)],
+        ("F", 1): [later(final, 2, 0), later(release, "a2")],
+        ("D", 2): [later(final, 2, 1)],
+        ("E", 1): [own_r],
+        ("S", 4): [later(compare, 6), later(weigh, 3), lambda: release(CB[6][0])],
+    })
+    final(3, 0); compare(7); final(3, 1); compare(8); weigh(4); release(WB[3]); release(CB[7][0])
+    gather(1, 6, 1, 2)
+    fused(1, 6); final(4, 0); release(WB[4])
+    lowest(T.nl0[:, 0:R], "nl0", T.r1, R1)
+    final(4, 1)
+    gather(1, 7, 1, 1)
+    act(T.sq[:], T.r1[:, 0:R], ["r1.own"], ["sq"], F.Square)
     minus_r(T.rj1, "rj1", T.r1, R1)
-    compare(6); compare(7); compare(8); weigh(3)
-    opened(1, 6); opened(2, 2)
-    lowest(T.nl0[:], "nl0", T.r1, R1)
-    final(3, 0)
-    opened(2, 3)
-    final(3, 1)
-    gather(1, 7); gather(1, 6)
-    fused(1, 7); fused(1, 6); direct(1, 7); total(1, 7, [0]); fused(1, 8); direct(1, 6); second(1, 6)
-    total(1, 8, [0])
-    act(row("x2"), row(BANKS[1][7]), ["P" + BANKS[1][7]], ["Px2"], scale=-1.0)
-    total(1, 6, [0, 2])
-    opened(2, 4)
+    direct(1, 6); total(1, 6); second(1, 6); fused(1, 7); direct(1, 7); total(1, 7)
+    evict(1, 6, None, None)
+    fused(1, 8); total(1, 8)
+    release("x2")
+    X2[2] = X2[3] = BANKS[1][7]
+    newton(1)
+    op("g", lambda: g.affine_select(T.nl0[:, R:2 * R], T.nl0[:, 0:R], [[0, R]], A.is_equal, 0.0, 0, 0), ["nl0"], ["nl02"])
 
-    r1own, r2own = (T.r1[:, 0:R], "r1.own"), (T.r2[:, 0:R], "r2.own")
-
-    def step_r():
-        newton(1, 0, *r1own); newton(1, 1, None, None)
-
-    def send_r():
-        newton(1, 2, *r1own, *r2own); rsend()
-
-    nw = CFG["newton"]
-    items(2, upper, up(3), merged(ships(3), opens(2, (0, 5), (2, 7), (3, 6)), opens(3, (4, 6), (5, 7)),
-                                  {nw[0]: [step_r], nw[1]: [send_r]}), CFG["lag2"])
-    gather(2, 7); gather(2, 6)
-    fused(2, 8); total(2, 8, [0]); fused(2, 7); direct(2, 7); total(2, 7, [0])
+    uppers(2, up(2), {("G", 0): [later(new_r, 1, T.r2[:, 0:R], "r2.own"), send_r],
+                      ("D", 3): [later(release, BANKS[1][9])], ("E", 1): [later(gather, 2, 7, 1, 1)],
+                      ("S", 3): [later(fused, 2, 8), later(total, 2, 8)]})
+    gather(2, 6, 1, 2)
+    fused(2, 7); direct(2, 7); total(2, 7); fused(2, 6)
+    act(T.sq[:], T.r2[:, 0:R], ["r2.own"], ["sq"], F.Square)
     minus_r(T.rj2, "rj2", T.r2, R2)
-    fused(2, 6); direct(2, 6); second(2, 6); total(2, 6, [0, 2])
-    scale(2, 8, T.rj1, "rj1", row("x1"), "Px1")
-    opened(3, 0)
-    scale(2, 7, T.rj1, "rj1", row("x2"), "Px2")
-    opened(3, 1)
+    for c, (x, y) in enumerate(((k2, k0), (k0, k1), (k1, k2), (k2, k0))):
+        tt(third(T.cmpx, c), x, y, A.is_gt, key, ["cmpx%d" % c])
     lowest(T.l3[:, 0:R], "l30", T.r2, R2)
-    newton(2, 0, *r2own)
-    newton(2, 1, None, None)
+    direct(2, 6); total(2, 6); second(2, 6)
+    tt(T.rk2[:], T.cmpx[:, 24:96], T.cmpx[:, 0:72], A.subtract, ["cmpx%d" % c for c in range(4)], ["rk2"])
+    scale(2, 8, T.rj1, "rj1", row("x1"), "Px1")
+    tt(T.rk3[:], T.rk2[:], T.nvf[:], A.add, ["rk2", "nvf"], ["rk3"])
+    scale(2, 7, T.rj1, "rj1", row(X2[3]), "P" + X2[3])
+    evict(2, 6, None, None)
+    ts(T.unperm[:], T.rk3[:], float(R), R + 0.25, A.mult, A.add, ["rk3"], ["unperm"])
 
     def out(c0, c1, keys):
         dma("y", T.y[:, c0:c1], T.yy[:, c0:c1], keys, ["y%d" % c0])
 
-    def ys(i):
+    def store(i):
         s = 4 + i if i < 6 else 3
-        return (T.yy[:, s * R:(s + 1) * R], "yy%d" % s) if i < 7 else None
+        cuts = (0, R // 2, R) if i in CFG["halves"] else (0, R)
+        for c0, c1 in zip(cuts, cuts[1:]):
+            evict(3, i, T.yy[:, s * R + c0:s * R + c1], "yy%d.%d" % (s, c0), c0, c1)
+            out(s * R + c0, s * R + c1, ["yy%d.%d" % (s, c0)])
 
     def lower():
         act(T.yy[:, 0:3 * R], T.l3[:, 0:3 * R].indirect(T.unperm[:, 0:72]), ["l30", "l31", "l32", "unperm"], ["yyl"], scale=-1.0)
         out(0, 3 * R, ["yyl"])
 
-    def last_r():
-        newton(2, 2, T.r2[:, 0:R], "r2.own", T.r3[:], "r3")
-        dma("y", T.inv[:], T.r3[:], ["r3"], ["inv"])
-
-    extra = {("E", i): [later(out, s * R, (s + 1) * R, ["yy%d" % s])] for i, s in enumerate((4, 5, 6, 7, 8, 9, 3))}
-    extra["F", 8] = [last_r, later(opened, 3, 5)]
-    extra["E", 8] = [later(scale, 3, 8, T.rj2, "rj2", T.l3[:, R:2 * R], "l31"), later(opened, 3, 2)]
-    extra["E", 7] = [later(scale, 3, 7, T.rj2, "rj2", T.l3[:, 2 * R:3 * R], "l32"), later(opened, 3, 3)]
-    extra["E", 6].append(later(opened, 3, 4))
-    extra["E", CFG["low"]].append(lower)
-    items(3, rest + upper, ys, extra, CFG["lag3"])
+    gather(3, 7, 1, 1); gather(3, 6, 1, 2); gather(3, 0, 1, 2)
+    fused(3, 8); total(3, 8); fused(3, 7); direct(3, 7); total(3, 7)
+    newton(2)
+    fused(3, 6); direct(3, 6); total(3, 6)
+    new_r(2, T.r3[:], "r3")
+    dma("y", T.inv[:], T.r3[:], ["r3"], ["inv"])
+    scale(3, 8, T.rj2, "rj2", T.l3[:, R:2 * R], "l31")
+    second(3, 6)
+    scale(3, 7, T.rj2, "rj2", T.l3[:, 2 * R:3 * R], "l32")
+    fused(3, 0, 2)
+    store(6)
+    uppers(3, store, {("G", 0): [lower], ("D", 1): [later(release, BANKS[2][9])]}, begun=True)
 
     for q in ("v", "s", "t", "g", "sent"):
         wait("g", (q, cnt[q], {}))
-    for a in sent:
-        wait("g", ("a_" + a, arrive, {}))
+    for a in ARR:
+        wait("g", ("a_" + a, arrive[a], {}))
     for i in range(cnt["d"]):
         wait("g", ("d%d" % i, 16, {}))

from concourse.bass import DstId, RemoteDMATransfer
from concourse.mybir import AluOpType, ActivationFunctionType

R, H, NB = 384, 64, 3
HB = 8 * R
HS = 8 * H
WN = HB + NB * HS
ZC = R + NB * H
CFG = {
    "far": (5,), "halves": (5,), "gu": 28,
    "eng": {"": (4, 4), "c0": (2, 2)},
}


def _sb(dtype, **shapes):
    return {k: ("sbuf", [128] + list(v), dtype) for k, v in shapes.items()}


SCRATCH = {}
SCRATCH.update(_sb("int32", colraw=[R], shp=[12], spt=[72], pi=[1], pt=[2], nvi=[72], ki=[72], sps=[72], blk=[72],
                   tsl=[72], cs=[72]))
SCRATCH.update(_sb("uint16", shp16=[12], vl=[84], lb=[24], list2=[72], prm=[72], unperm=[72], rl=[72], ls=[576]))
SCRATCH.update(_sb("float16", csg=[NB * H], colh=[12, 2, 16], q4=[4 * 128], sel=[2 * 128], c3=[72, 9], off=[72], idh=[128],
                   negh=[128], ab=[2 * 432], gu=[72 * 16], tu=[72, 16]))
SCRATCH.update(_sb("bfloat16", vsend=[NB * 7 * H], eq=[24, 24, 6], tb=[128], ti=[128], tm=[128], idb=[128], negb=[128],
                   idw=[6 * 128], zero=[432], two=[128], al=[3 * R], nal=[4 * R], w1=[WN]))
SCRATCH.update(_sb("float32", cw=[2 * ZC], csend=[2 * NB * H], pf=[8], shpf=[12], stg=[3, 7, 4], ext=[72], neg2=[128], sq=[R],
                   cl=[24, 16], cmpx=[96], nvf=[72], spf=[72], srt=[72], tmp=[72], tsf=[72], base=[72], ta=[72],
                   istr=[72], bq2=[3, 2, 24], sd2=[3, 2, 24], fin=[576], rk2=[72], rk3=[72],
                   negf=[128], idf=[128], w2=[WN], w3=[WN], r1=[ZC], r2=[ZC], r3=[R], rsend=[NB * H],
                   rj1=[2 * R], rj2=[2 * R], nl0=[2 * R], l3=[3 * R], gg=[15 * R], p0=[9 * R], p2=[7 * R], snd2=[NB * 6 * H],
                   snd3=[NB * 6 * H], yy=[10 * R]))
for _n in ("x1", "x2", "a0", "a1", "a2", "a4", "a5"):
    SCRATCH[_n] = ("psum", [128, 512], "float32")
SCRATCH["a3"] = ("psum", [128, 16, 32], "float32")
ARR = ["c0", "v0", "r2"] + ["x%d%d" % (k, i) for k in (2, 3) for i in range(3)]
SEMAPHORES = ["v", "s", "t", "g", "sent"] + ["a_" + a for a in ARR] + ["d%d" % i for i in range(24)]


def rank_program(g, core, T, topo):
    rank = T.rank_of(core)
    if rank is None:
        return
    A = AluOpType
    F = ActivationFunctionType
    N = len(T.cores)
    Q = {"v": g.vector, "s": g.scalar, "t": g.tensor, "g": g, "y": g.sync}
    cnt = {"v": 0, "s": 0, "t": 0, "g": 0, "sent": 0, "d": 0}
    clock = {q: {} for q in Q}
    writer, readers = {}, {}

    def wait(q, tok):
        sem, n, clk = tok[0], tok[1], tok[2]
        c = clock[q]
        if c.get(sem, 0) >= n:
            return
        Q[q].wait_ge(T.sem[sem], n)
        c[sem] = n
        for k in clk:
            if c.get(k, 0) < clk[k]:
                c[k] = clk[k]

    def before(q, rd, wr, dma):
        need = []
        for k in rd:
            if k in writer:
                need.append(writer[k])
            if k[0] == "P":
                need += [t for t in readers.get(k, []) if t[3] != q]
        for k in wr:
            if k in writer and (dma or writer[k][3] != q):
                need.append(writer[k])
            need += readers.get(k, [])
        need.sort(key=lambda t: -t[1])
        for t in need:
            wait(q, t)

    def after(tok, rd, wr):
        for k in rd:
            readers.setdefault(k, []).append(tok)
        for k in wr:
            writer[k] = tok
            readers[k] = []

    def op(q, call, rd, wr):
        before(q, rd, wr, False)
        cnt[q] += 1
        call().then_inc(T.sem[q], 1)
        after((q, cnt[q], dict(clock[q]), q), rd, wr)

    def mm(calls, rd, wr, each=False, start=True, stop=True):
        before("t", rd, wr, False)
        for i, (o, l, r) in enumerate(calls):
            ins = g.tensor.matmul(o, l, r, each or (start and i == 0), each or (stop and i == len(calls) - 1))
        cnt["t"] += 1
        ins.then_inc(T.sem.t, 1)
        after(("t", cnt["t"], dict(clock["t"]), "t"), rd, wr)

    def dma(q, out, in_, rd, wr):
        before(q, rd, wr, True)
        sem = "d%d" % cnt["d"]
        cnt["d"] += 1
        Q[q].dma_start(out, in_).then_inc(T.sem[sem], 16)
        after((sem, 16, dict(clock[q]), "dma"), rd, wr)

    def plan(src, name):
        dsts = [c for c in T.cores if c != src]
        far = [c for c in dsts if topo.chip(c) != topo.chip(src)]
        near = [c for c in dsts if c not in far]
        used, out = [], {}
        for grp, n in zip((far, near), CFG["eng"].get(name, CFG["eng"][""])):
            if not grp:
                continue
            free = [e for e in topo.engines(src, grp[0]) if e not in used]
            while n * len(grp) > len(free):
                n //= 2
            step = len(free) // n
            for i, c in enumerate(grp):
                out[c] = free[i * (step // len(grp))::step][:n]
            used += free
        return out

    others = [p for p in range(N) if p != rank]
    arrive = {a: sum(len(plan(T.cores[p], a)[core]) for p in others) for a in ARR}

    def send(name, src, width, dst, rd):
        before("g", rd, [], True)
        tr = []
        mine = plan(core, name)
        for b, p in enumerate(others):
            c = T.cores[p]
            rid, pid = topo.addr(c)[0:2]
            me = rank if rank < p else rank - 1
            m = sum(1 << e for e in mine[c])
            tr.append(RemoteDMATransfer(dst_ids=[DstId(rid=rid, pnc=pid)], dma_engine_mask=m,
                                        remote_sem=T.sem["a_" + name], src=src(b * width, (b + 1) * width), dst=dst(me)))
            cnt["sent"] += len(mine[c])
        g.remote_dma_fused(tr, local_sem=T.sem.sent)

    for a in ARR:
        writer["arr." + a] = ("a_" + a, arrive[a], {}, "far")

    V, S = g.vector, g.scalar

    def tt(out, a, b, o, rd, wr):
        op("v", lambda: V.tensor_tensor(out, a, b, o), rd, wr)

    def ts(out, a, s1, s2, o0, o1, rd, wr):
        if o1 is None:
            op("v", lambda: V.tensor_scalar(out, a, s1, None, o0), rd, wr)
        else:
            op("v", lambda: V.tensor_scalar(out, a, s1, s2, o0, o1), rd, wr)

    def cp(out, a, rd, wr):
        op("v", lambda: V.tensor_copy(out, a), rd, wr)

    def act(out, a, rd, wr, f=F.Identity, scale=1.0, bias=0.0):
        if scale == 1.0 and bias == 0.0:
            op("s", lambda: S.activation(out, a, F.Copy if f == F.Identity else f), rd, wr)
        else:
            op("s", lambda: S.activation(out, a, f, bias=bias, scale=scale), rd, wr)

    def third(buf, t):
        return buf[:, 24 * t:24 * t + 24]

    BANK = {n: T[n] for n in ("x1", "x2", "a0", "a1", "a2", "a3", "a4", "a5")}

    def row(n, c0=0, c1=R):
        return T.a3[:, c0 // 32:c1 // 32, :] if n == "a3" else BANK[n][:, c0:c1]

    dma("y", T.colraw[0:128:2, :], T.col[:, 2 * R:10 * R], [], ["colA"])
    dma("s", T.shp[:], T.ship[:], [], ["shp"])
    dma("s", T.colraw[1:128:2, :], T.col[:, 0:8 * R], [], ["colB"])
    dma("y", T.spt[:], T.spot[:], [], ["spt"])
    dma("y", T.w1[:, R:HB], T.val[:, 3 * R:10 * R], [], ["w1.own"])
    dma("y", T.al[:], T.val[:, 0:3 * R], [], ["al"])

    def table(buf, key, pattern):
        op("g", lambda: g.iota(buf[:], pattern, 0, -1, allow_small_or_imprecise_dtypes=True), [], [key])

    table(T.tb, "tb", [[32, 4], [0, 2], [1, 16]])
    op("g", lambda: g.iota(T.pi[:], [[0, 1]], 0, 1), [], ["pi"])
    table(T.ti, "ti", [[1, 128]])
    table(T.tm, "tm", [[32, 4], [128, 2], [1, 16]])
    op("g", lambda: g.iota(T.nvi[:], [[0, 3], [16, 24]], 0, 1), [], ["nvi"])

    def move(e, f):
        return T.q4[:, (2 * e + f) * 128:(2 * e + f + 1) * 128]

    def both(e):
        return T.sel[:, e * 128:(e + 1) * 128]

    def diag(q, out, key, x):
        if q == "s":
            act(out, T.idb[:], ["idb"], [key], scale=x)
        else:
            ts(out, T.ti[:], 0.0, x, A.is_equal, A.mult, ["ti"], [key])

    def weights(q, ws):
        for w in ws:
            diag(q, T.idw[:, w * 128:(w + 1) * 128], "idw%d" % w, float(H * (w + 2)))

    op("v", lambda: V.memset(T.zero[:], 0.0), [], ["zero"])
    for e in range(2):
        ts(both(e), T.tb[:], -16.0 * e, None, A.is_equal, None, ["tb"], ["sel%d" % e])
    ts(T.pt[:, 0:1], T.pi[:], 4, None, A.logical_shift_right, None, ["pi"], ["pt0"])
    ts(T.pt[:, 1:2], T.pi[:], 4, 1, A.logical_shift_right, A.bitwise_and, ["pi"], ["pt1"])
    M1, PH = [T.pf[:, i:i + 1] for i in range(2)]
    diag("v", T.idb[:], "idb", 1.0)
    diag("v", T.idh[:], "idh", 1.0)
    ts(PH, T.pt[:, 0:1], 16.0, None, A.mult, None, ["pt0"], ["ph"])
    ts(M1, T.pt[:, 1:2], 1.0, None, A.mult, None, ["pt1"], ["m1"])
    weights("s", (0, 1, 2))
    for e in range(2):
        for f in range(2):
            ts(move(e, f), T.tm[:], 128.0 * f - 16.0 * e, None, A.is_equal, None, ["tm"], ["q%d%d" % (e, f)])
    mv = ["q00", "q01", "q10", "q11"]
    ts(T.nvf[:], T.nvi[:], PH, 1.0 / R, A.subtract, A.mult, ["nvi", "ph"], ["nvf"])
    for buf, key, x in ((T.idf, "idf", 1.0), (T.negf, "negf", -1.0), (T.neg2, "neg2", -2.0)):
        diag("s", buf[:], key, x)

    col = ["colA", "colB"]
    cp(T.shpf[:], T.shp[:], ["shp"], ["shpf"])
    cp(T.shp16[:], T.shp[:], ["shp"], ["shp16"])
    stg = ["stg%d" % w for w in range(7)]

    def planes(ws):
        for w in ws:
            act(T.stg[:, :, w, :], T.shpf[:], ["shpf"], [stg[w]], bias=float(w * R))

    planes(range(4))
    cp(T.csg[:], T.colraw[:, 0:R].indirect(T.shp16[:, 0:12]), col + ["shp16"], ["csg"])
    mm([(T.a0[:, e:2 * NB * H:2], both(e), T.csg[:]) for e in range(2)], ["csg", "sel0", "sel1"], ["Pa0"], True)
    act(T.csend[:], T.a0[:, 0:2 * NB * H], ["Pa0"], ["csend"])
    send("c0", lambda a, b: T.csend[:, a:b], 2 * H, lambda b: T.cw[:, 2 * (R + b * H):2 * (R + (b + 1) * H)], ["csend"])
    cp(T.colh[:], T.colraw[:], col, ["colh"])
    for e in range(2):
        mm([(T.a3[:, 0:12, 16 * e:16 * e + 16], move(e, f), T.colh[:, :, f, :]) for f in range(2)], mv + ["colh"], ["Pa3"])
    for e in range(2):
        mm([(row("a%d" % (1 + e)), both(e), T.colh[:])], ["colh", "sel%d" % e], ["Pa%d" % (1 + e)])
    for t in range(3):
        ts(third(T.spf, t), third(T.spt, t), 1.0 / 1024, 3.0 + t / 4096.0, A.mult, A.add, ["spt"], ["spf%d" % t])
    planes(range(4, 7))
    weights("v", (3, 4, 5))
    op("v", lambda: V.transpose(T.cl[:], row("a3")), ["Pa3"], ["cl"])
    act(T.cw[:, 1:2 * R:2], row("a2"), ["Pa2"], ["cw1"])

    JOINS = [3] * 7 + [2, 1]
    FAR = CFG["far"]
    CB = [("x1", 0), ("x2", 0), ("a0", 0), ("a1", 0), ("a2", 0), ("a4", 0), None, None, None]

    def spread(i):
        s = (i + 1 if i < 6 else 0) if i < 7 else 15 - i
        bk, o = CB[i]
        calls = [(BANK[bk][:, o + w:o + 144 * JOINS[i]:6], T.idh[:], T.c3[:, 0:24 * JOINS[i], s]) for w in range(6)]
        rd = ["idh"] + (["c30", "c31", "c32"] if i < 7 else ["c3a", "c3b", "c3c"])
        if i in FAR:
            mm([(BANK[bk][:, 0:432], T.idb[:], T.zero[:])] + calls, rd + ["idb", "zero"], ["P" + bk], stop=False)
        else:
            mm(calls, rd, ["P" + bk], True)

    k0, k1, k2 = [third(T.ext, t) for t in range(3)]
    s0, s1, s2 = [third(T.srt, t) for t in range(3)]
    m0, m1, m2 = [third(T.tmp, t) for t in range(3)]
    diag("v", T.negb[:], "negb", -1.0)
    diag("v", T.negh[:], "negh", -1.0)
    diag("v", T.two[:], "two", 2.0)
    for t in range(3):
        tt(third(T.ext, t), T.cl[:, :, 2 * t + 1], third(T.spf, t), A.add, ["cl", "spf%d" % t], ["k%d" % t])
    key = ["k0", "k1", "k2"]
    cp(T.c3[:, 0:24, 0:7], T.cl[:, :, 2:16:2], ["cl"], ["c30"])
    tt(m1, k0, k1, A.max, key[0:2], ["tm1"])
    tt(m0, k0, k1, A.min, key[0:2], ["tm0"])
    cp(T.vl[:], T.stg[:], stg, ["vl"])
    cp(T.c3[:, 24:48, 0:7], T.cl[:, :, 2:16:2], ["cl"], ["c31"])
    act(T.vsend[:], T.w1[:, R:HB].indirect(T.vl[:, 0:84]), ["w1.own", "vl"], ["vsend"])
    send("v0", lambda a, b: T.vsend[:, a:b], 7 * H, lambda b: T.w1[:, HB + b * HS + H:HB + (b + 1) * HS], ["vsend"])
    for k, W, n in ((1, T.w1, 1), (2, T.w2, 2), (3, T.w3, 2)):
        op("g", lambda: g.iota(W[:, 0:n * R], [[0, n * R]], 0, 0, allow_small_or_imprecise_dtypes=True), [], ["w%d.z0" % k])
        for b in range(NB):
            op("g", lambda: g.iota(W[:, HB + b * HS:HB + b * HS + n * H], [[0, n * H]], 0, 0,
                                   allow_small_or_imprecise_dtypes=True), [], ["w%d.z%d" % (k, b + 1)])
    tt(m2, m1, k2, A.min, ["tm1", "k2"], ["tm2"])
    tt(s2, m1, k2, A.max, ["tm1", "k2"], ["s2"])
    tt(s0, m0, k2, A.min, ["tm0", "k2"], ["s0"])
    tt(s1, m0, m2, A.max, ["tm0", "tm2"], ["s1"])
    cp(T.cw[:, 0:2 * R:2], row("a1"), ["Pa1"], ["cw0"])
    ts(T.ki[:], T.srt[:], 4096.0, None, A.mult, None, ["s0", "s1", "s2"], ["ki"])
    cp(T.lb[:], T.stg[:, :, 0:2, :], stg, ["lb"])
    cp(T.c3[:, 48:72, 0:7], T.cl[:, :, 2:16:2], ["cl"], ["c32"])
    for i in (0, 1, 2):
        spread(i)
    ts(T.sps[:], T.ki[:], 2, 1023, A.logical_shift_right, A.bitwise_and, ["ki"], ["sps"])
    ts(T.tsl[:], T.ki[:], 3, None, A.bitwise_and, None, ["ki"], ["tsl"])
    ts(T.blk[:], T.ki[:], 8, 15, A.logical_shift_right, A.bitwise_and, ["ki"], ["blk"])
    ts(T.off[:], T.sps[:], 2.0, M1, A.mult, A.add, ["sps", "m1"], ["off"])
    for e in range(2):
        mm([(T.a4[:, e:72:2], move(e, f), T.off[:, f:72:2]) for f in range(2)], mv + ["off"], ["Pa4"])
    tt(T.tsf[:], T.tsl[:], T.nvf[:], A.add, ["tsl", "nvf"], ["tsf"])
    ts(T.ta[:], T.blk[:], 6.0, float(HS - H), A.is_ge, A.mult, ["blk"], ["ta"])
    ts(T.istr[:], T.blk[:], 6.0, H / R, A.is_ge, A.max, ["blk"], ["istr"])
    ts(T.prm[:], T.tsf[:], float(R), 0.25, A.mult, A.add, ["tsf"], ["prm"])
    tt(T.ta[:], T.ta[:], T.blk[:], A.mult, ["ta", "blk"], ["ta"])
    cp(T.list2[:], T.a4[:, 0:72], ["Pa4"], ["list2"])
    act(T.nal[:, R:4 * R], T.al[:, 0:3 * R].indirect(T.prm[:, 0:72]), ["al", "prm"], ["nal"], scale=-1.0)
    for i in (3, 4, 5):
        spread(i)
    ts(T.sd2[:, :, 0, :], T.blk[:], 6.0, H / R, A.is_lt, A.max, ["blk"], ["sd0"])
    tt(T.base[:], T.ta[:], T.sps[:], A.add, ["ta", "sps"], ["base"])
    ts(T.sd2[:, :, 1, :], T.blk[:], 6.0, H / R, A.is_lt, A.max, ["blk"], ["sd1"])
    ts(T.cs[:], T.ki[:], 12, None, A.logical_shift_right, None, ["ki"], ["cs"])
    tt(T.bq2[:, :, 0, :], T.base[:], T.istr[:], A.mult, ["base", "istr"], ["bq0"])

    cwk = ["cw0", "cw1", "arr.c0", "list2"]
    cut = (0, CFG["gu"], (72 + CFG["gu"]) // 4 * 2, 72)
    for j in range(3):
        (act if j else cp)(T.gu[:, 16 * cut[j]:16 * cut[j + 1]], T.cw[:, 0:2 * ZC].indirect(T.list2[:, cut[j]:cut[j + 1]]), cwk, ["gu%d" % j])
    cp(T.nal[:, 0:R], T.nal[:, R:2 * R], ["nal"], ["nal2"])
    for j in range(3):
        op("v", lambda: V.transpose(T.tu[:, cut[j]:cut[j + 1], :], T.gu[:, 16 * cut[j]:16 * cut[j + 1]]), ["gu%d" % j], ["tu%d" % j])
    cp(T.rl[:], T.sps[:], ["sps"], ["rl"])
    tt(T.bq2[:, :, 1, :], T.base[:], T.istr[:], A.mult, ["base", "istr"], ["bq1"])

    def block(i, j):
        return 6 * (i // 2) + 2 * j + i % 2 if i < 6 else (18, 21, 23)[i - 6] + j

    def compare(i):
        n, step = JOINS[i], 2 if i < 6 else 1
        bk, o = CB[i]
        tt(T.eq[:, block(i, 0):block(i, n - 1) + 1:step, :, :], BANK[bk][:, o:o + 144 * n], T.tu[:, 0:24 * n, 4:16:2], A.is_equal,
           ["P" + bk, "tu0", "tu1", "tu2"], ["eq%d" % i])

    def differ(i):
        bk, c = CB[i][0], 432 * (i % 2)
        mm([(BANK[bk][:, 0:432], T.negh[:], T.tu[:, :, 4:16:2])], ["negh", "tu0", "tu1", "tu2", "P" + bk], ["P" + bk], start=False)
        act(T.ab[:, c:c + 432], BANK[bk][:, 0:432], ["P" + bk], ["ab%d" % i], F.Abs)
        act(T.eq[:, block(i, 0):block(i, 2) + 1:2, :, :], T.ab[:, c:c + 432], ["ab%d" % i], ["eq%d" % i], F.Relu, scale=-1.0, bias=1.0)

    GROUP = [(0, 1), (2, 3), (4, 5), (6,), (7, 8)]
    WB = ["a5", "a0", "a2", None, None]

    def span(lg):
        return block(GROUP[lg][0], 0), sum(JOINS[i] for i in GROUP[lg])

    def weigh(lg):
        B = BANK[WB[lg]]
        o, n = span(lg)
        calls = [(B[:, 0:24 * n], T.idw[:, w * 128:(w + 1) * 128], T.eq[:, o:o + n, :, w]) for w in range(6)]
        if lg < 3:
            calls += [(B[:, 0:144], T.idf[:], T.bq2[:])]
        else:
            calls += [(B[:, 24 * (block(i, 0) - o):24 * (block(i, 0) - o + JOINS[i])], T.idf[:], T.bq2[:, 0:JOINS[i], 0, :])
                      for i in GROUP[lg]]
        mm(calls, ["eq%d" % i for i in GROUP[lg]] + ["idw%d" % w for w in range(6)] + ["idf", "bq0", "bq1"], ["P" + WB[lg]])

    def final(lg, step):
        o, n = span(lg)
        c = slice(24 * o, 24 * (o + n))
        if step == 0:
            parts = [(0, n, T.sd2[:])] if lg < 3 else [(block(i, 0) - o, JOINS[i], T.sd2[:, 0:JOINS[i], 0, :]) for i in GROUP[lg]]
            for x, m, sd in parts:
                tt(T.fin[:, 24 * (o + x):24 * (o + x + m)], BANK[WB[lg]][:, 24 * x:24 * (x + m)], sd, A.mult,
                   ["P" + WB[lg], "sd0", "sd1"], ["fin%d.%d" % (lg, x)])
        else:
            ts(T.ls[:, c], T.fin[:, c], float(R // H), 0.25, A.mult, A.add, ["fin%d.%d" % (lg, x) for x in (0, 2)], ["ls%d" % lg])

    WIN = {1: T.w1, 2: T.w2, 3: T.w3}
    WK = {1: ["w1.own", "arr.v0"] + ["w1.z%d" % i for i in range(4)]}
    for k in (2, 3):
        WK[k] = (["w%d.u%d" % (k, w) for w in range(6)] + ["w%d.z%d" % (k, i) for i in range(4)]
                 + ["arr.x%d%d" % (k, i) for i in range(3)])
    NL0 = {1: (T.nal, ["nal2", "nal"]), 2: (T.nal, ["nal2", "nal"]), 3: (T.nl0, ["nl0", "nl02"])}
    BANKS = {1: {8: "x1"}, 2: {}, 3: {}}
    queue = ([(1, i) for i in range(6)] + [("c", 6), ("c", 7), ("w", 3), ("w", 4), (1, 7), (1, 6), (1, 9)]
             + [(2, i) for i in (0, 1, 2, 3, 4, 5, 8, 7, 6, 9)] + [(3, i) for i in (8, 7, 6, 0, 1, 2, 3, 4, 5)])
    free = []
    X2 = {1: "x2"}

    def release(b):
        free.append(b)
        while free and queue:
            k, i = queue[0]
            fit = [x for x in free if x != "a3" or k not in ("c", "w")]
            if not fit:
                return
            queue.pop(0)
            free.remove(fit[0])
            if k == "c":
                for j in ((6,), (7, 8))[i - 6]:
                    CB[j] = (fit[0], 288 if j == 8 else 0)
                    spread(j)
            elif k == "w":
                WB[i] = fit[0]
            else:
                BANKS[k][i] = fit[0]
                if i != 8:
                    opened(k, i)

    def window(k, i, j, n):
        o = 24 * block(i, j)
        return WIN[k][:, 0:WN].indirect(T.ls[:, o:o + 24 * n]), WK[k] + ["ls%d" % (i // 2 if i < 7 else 4)]

    def got(i, j):
        c = 4 * (i // 2) + 2 * (j - 1) + i % 2 if i < 6 else (12, 14)[i - 6] + j - 1
        return c * R, "g%d" % c

    def gather(k, i, j, n):
        src, rd = window(k, i, j, n)
        c = got(i, j)[0]
        act(T.gg[:, c:c + n * R], src, rd, ["g%d" % (c // R + x) for x in range(n)])

    def fused(k, i, n=1):
        src, rd = window(k, i, 0, n)
        tt(T.p0[:, i * R:(i + n) * R], src, NL0[k][0][:, 0:n * R], A.mult, rd + NL0[k][1][0:n], ["p0%d" % x for x in range(i, i + n)])

    def prod(i, j):
        return (T.p0 if j == 0 else T.p2)[:, i * R:(i + 1) * R], "p%d%d" % (j, i)

    def opened(k, i):
        b = BANKS[k][i]
        mm([(row(b), T.idb[:], T.zero[:, 0:R])], ["idb", "zero"], ["P" + b], stop=False)

    def direct(k, i):
        b = BANKS[k][i]
        c, uk = got(i, 1)
        tt(row(b), T.gg[:, c:c + R], row("x1"), A.mult, [uk, "Px1"], ["P" + b])

    def second(k, i):
        c, uk = got(i, 2)
        tt(prod(i, 2)[0], T.gg[:, c:c + R], row(X2[k]), A.mult, [uk, "P" + X2[k]], [prod(i, 2)[1]])

    def total(k, i):
        b = BANKS[k][i]
        if i < 7:
            c = (2 + i) * R if i < 6 else R
            calls = [(row(b), T.idb[:], T.w1[:, c:c + R])]
        else:
            calls = [(row(b), T.idb[:] if b == "x1" else T.negb[:], T.nal[:, (10 - i) * R:(11 - i) * R])]
        calls += [(row(b), T.negf[:] if b == "x1" else T.idf[:], prod(i, 0)[0])]
        mm(calls, ["idb", "negb", "idf", "negf", "nal", "w1.own", prod(i, 0)[1]] + ([] if i == 8 else ["P" + b]),
           ["P" + b], start=(i == 8))

    def evict(k, i, out, key, c0=0, c1=R):
        b = BANKS[k][i]
        tt(out if key else row(b), row(b, c0, c1), T.p2[:, i * R + c0:i * R + c1], A.subtract if k == 2 else A.add,
           ["P" + b, prod(i, 2)[1]], [key or "P" + b])
        if key and c1 == R:
            release(b)

    def scale(k, i, rj, rk, out, ok):
        b = BANKS[k][i]
        tt(out, row(b), rj[:, (8 - i) * R:(9 - i) * R], A.mult, ["P" + b, rk], [ok])
        release(b)

    def ship(k, c):
        SB = T.snd2 if k == 2 else T.snd3
        w0, o = 2 * c, NB * 2 * c * H
        key = "snd%d%d" % (k, c)
        act(SB[:, o:o + NB * 2 * H], WIN[k][:, (2 + w0) * R:(4 + w0) * R].indirect(T.lb[:, 0:24]),
            ["w%d.u%d" % (k, w0), "w%d.u%d" % (k, w0 + 1), "lb"], [key])
        send("x%d%d" % (k, c), lambda a, b: SB[:, o + a:o + b], 2 * H,
             lambda b: WIN[k][:, HB + b * HS + (2 + w0) * H:HB + b * HS + (4 + w0) * H], [key])

    def newton(k):
        b, n = BANKS[k][6], BANKS[k][9]
        tt(row(n), row(b), T.sq[:], A.mult, ["P" + b, "sq"], ["P" + n])
        release(b)
        if k == 1:
            mm([(row(n), T.two[:], T.w1[:, R:2 * R])], ["two", "w1.own", "P" + n], ["P" + n], start=False)
        else:
            mm([(row(n), T.neg2[:], T.r2[:, 0:R])], ["neg2", "r2.own", "P" + n], ["P" + n], start=False)

    def new_r(k, out, ok):
        n = BANKS[k][9]
        act(out, row(n), ["P" + n], [ok], scale=-1.0, bias=4.0 if k == 1 else 0.0)

    def later(f, *a):
        return lambda: f(*a)

    def uppers(k, leave, extra, begun=False):
        def also(x, p):
            for f in extra.get((x, p), ()):
                f()

        def directs(p):
            for i in (2 * p, 2 * p + 1):
                direct(k, i); total(k, i)
                also("D", i)

        if not begun:
            gather(k, 0, 1, 2)
            if k == 1:
                gather(k, 0, 2, 2)
            fused(k, 0, 2)
        also("F", 0)
        directs(0)
        gather(k, 2, 1, 2)
        if k > 1:
            gather(k, 0, 2, 2)
        also("G", 0)
        fused(k, 2, 2)
        also("F", 1)
        for p in range(3):
            if p < 2:
                directs(p + 1)
            if p == 0:
                gather(k, 4, 1, 2); gather(k, 2, 2, 2)
            for i in (2 * p, 2 * p + 1):
                second(k, i)
                also("S", i)
            for i in (2 * p, 2 * p + 1):
                leave(i)
            if p == 0:
                gather(k, 4, 2, 2)
                fused(k, 4, 2)
            also("E", p)

    def up(k):
        def leave(w):
            evict(k, w, WIN[k + 1][:, (2 + w) * R:(3 + w) * R], "w%d.u%d" % (k + 1, w))
            if w % 2:
                ship(k + 1, w // 2)
        return leave

    R1 = ["r1.own", "r1.0", "r1.1", "r1.2", "rl"]
    R2 = ["r2.own", "arr.r2", "rl"]

    def own_r():
        act(T.r1[:, 0:R], T.w1[:, R:2 * R], ["w1.own"], ["r1.own"], scale=-1.0, bias=2.0)

    def far_r():
        for b in range(NB):
            c = HB + b * HS + H
            ts(T.r1[:, R + b * H:R + (b + 1) * H], T.w1[:, c:c + H], -1.0, 2.0, A.mult, A.add, ["arr.v0"], ["r1.%d" % b])

    def send_r():
        act(T.rsend[:], T.r2[:, 0:R].indirect(T.shp16[:, 0:12]), ["r2.own", "shp16"], ["rsend"])
        send("r2", lambda a, b: T.rsend[:, a:b], H, lambda b: T.r2[:, R + b * H:R + (b + 1) * H], ["rsend"])

    def minus_r(out, key, tab, rd):
        act(out[:], tab[:, 0:ZC].indirect(T.rl[:, 24:72]), rd, [key], scale=-1.0)

    def lowest(out, key, tab, rd):
        tt(out, tab[:, 0:ZC].indirect(T.rl[:, 0:24]), T.nal[:, 0:R], A.mult, rd + ["nal2"], [key])

    for i in FAR:
        differ(i)
    compare(0); compare(1); weigh(0)
    for j in (1, 2):
        mm([(row("x%d" % j), T.idb[:], T.nal[:, (j + 1) * R:(j + 2) * R])], ["idb", "nal"], ["Px%d" % j])
    compare(2); compare(3); weigh(1)
    if 4 not in FAR:
        compare(4)
    final(0, 0)
    ts(T.c3[:, 0:24, 7], third(T.cs, 1), -3.0, None, A.add, None, ["cs"], ["c3a"])
    ts(T.c3[:, 0:24, 8], third(T.cs, 2), -3.0, None, A.add, None, ["cs"], ["c3b"])
    ts(T.c3[:, 24:48, 8], third(T.cs, 2), -3.0, None, A.add, None, ["cs"], ["c3c"])
    final(0, 1)
    far_r()
    release("a3"); release("a5")
    uppers(1, up(1), {
        ("F", 0): [later(final, 1, 0), later(release, "a0"), later(release, "a1"), later(weigh, 2), later(release, "a4")],
        ("D", 0): [later(final, 1, 1)],
        ("F", 1): [later(final, 2, 0), later(release, "a2")],
        ("D", 2): [later(final, 2, 1)],
        ("E", 1): [own_r],
        ("S", 4): [later(compare, 6), later(weigh, 3), lambda: release(CB[6][0])],
    })
    final(3, 0); compare(7); final(3, 1); compare(8); weigh(4); release(WB[3]); release(CB[7][0])
    gather(1, 6, 1, 2)
    fused(1, 6); final(4, 0); release(WB[4])
    lowest(T.nl0[:, 0:R], "nl0", T.r1, R1)
    final(4, 1)
    gather(1, 7, 1, 1)
    act(T.sq[:], T.r1[:, 0:R], ["r1.own"], ["sq"], F.Square)
    minus_r(T.rj1, "rj1", T.r1, R1)
    direct(1, 6); total(1, 6); second(1, 6); fused(1, 7); direct(1, 7); total(1, 7)
    evict(1, 6, None, None)
    fused(1, 8); total(1, 8)
    release("x2")
    X2[2] = X2[3] = BANKS[1][7]
    newton(1)
    op("g", lambda: g.affine_select(T.nl0[:, R:2 * R], T.nl0[:, 0:R], [[0, R]], A.is_equal, 0.0, 0, 0), ["nl0"], ["nl02"])

    uppers(2, up(2), {("G", 0): [later(new_r, 1, T.r2[:, 0:R], "r2.own"), send_r],
                      ("D", 3): [later(release, BANKS[1][9])], ("E", 1): [later(gather, 2, 7, 1, 1)],
                      ("S", 3): [later(fused, 2, 8), later(total, 2, 8)]})
    gather(2, 6, 1, 2)
    fused(2, 7); direct(2, 7); total(2, 7); fused(2, 6)
    act(T.sq[:], T.r2[:, 0:R], ["r2.own"], ["sq"], F.Square)
    minus_r(T.rj2, "rj2", T.r2, R2)
    for c, (x, y) in enumerate(((k2, k0), (k0, k1), (k1, k2), (k2, k0))):
        tt(third(T.cmpx, c), x, y, A.is_gt, key, ["cmpx%d" % c])
    lowest(T.l3[:, 0:R], "l30", T.r2, R2)
    direct(2, 6); total(2, 6); second(2, 6)
    tt(T.rk2[:], T.cmpx[:, 24:96], T.cmpx[:, 0:72], A.subtract, ["cmpx%d" % c for c in range(4)], ["rk2"])
    scale(2, 8, T.rj1, "rj1", row("x1"), "Px1")
    tt(T.rk3[:], T.rk2[:], T.nvf[:], A.add, ["rk2", "nvf"], ["rk3"])
    scale(2, 7, T.rj1, "rj1", row(X2[3]), "P" + X2[3])
    evict(2, 6, None, None)
    ts(T.unperm[:], T.rk3[:], float(R), R + 0.25, A.mult, A.add, ["rk3"], ["unperm"])

    def out(c0, c1, keys):
        dma("y", T.y[:, c0:c1], T.yy[:, c0:c1], keys, ["y%d" % c0])

    def store(i):
        s = 4 + i if i < 6 else 3
        cuts = (0, R // 2, R) if i in CFG["halves"] else (0, R)
        for c0, c1 in zip(cuts, cuts[1:]):
            evict(3, i, T.yy[:, s * R + c0:s * R + c1], "yy%d.%d" % (s, c0), c0, c1)
            out(s * R + c0, s * R + c1, ["yy%d.%d" % (s, c0)])

    def lower():
        act(T.yy[:, 0:3 * R], T.l3[:, 0:3 * R].indirect(T.unperm[:, 0:72]), ["l30", "l31", "l32", "unperm"], ["yyl"], scale=-1.0)
        out(0, 3 * R, ["yyl"])

    gather(3, 7, 1, 1); gather(3, 6, 1, 2); gather(3, 0, 1, 2)
    fused(3, 8); total(3, 8); fused(3, 7); direct(3, 7); total(3, 7)
    newton(2)
    fused(3, 6); direct(3, 6); total(3, 6)
    new_r(2, T.r3[:], "r3")
    dma("y", T.inv[:], T.r3[:], ["r3"], ["inv"])
    scale(3, 8, T.rj2, "rj2", T.l3[:, R:2 * R], "l31")
    second(3, 6)
    scale(3, 7, T.rj2, "rj2", T.l3[:, 2 * R:3 * R], "l32")
    fused(3, 0, 2)
    store(6)
    uppers(3, store, {("G", 0): [lower], ("D", 1): [later(release, BANKS[2][9])]}, begun=True)

    for q in ("v", "s", "t", "g", "sent"):
        wait("g", (q, cnt[q], {}))
    for a in ARR:
        wait("g", ("a_" + a, arrive[a], {}))
    for i in range(cnt["d"]):
        wait("g", ("d%d" % i, 16, {}))
